import numpy as np
import ml_dtypes


def mxq(x, axis, fmt="e4m3"):
    dtype, down = {"e4m3": (ml_dtypes.float8_e4m3fn, 7), "e5m2": (ml_dtypes.float8_e5m2, 14)}[fmt]
    v = np.moveaxis(np.asarray(x, np.float32).astype(ml_dtypes.bfloat16).astype(np.float64), axis, -1)
    blocks = v.reshape(v.shape[:-1] + (-1, 32))
    amax = np.abs(blocks).max(-1, keepdims=True)
    byte = np.maximum(np.where(amax > 0, np.frexp(amax)[1] - 1 + 127, 0) - down, 1)
    scale = np.exp2(byte - 127.0)
    codes = (blocks / scale).astype(np.float32).astype(dtype).astype(np.float64)
    return np.moveaxis((codes * scale).reshape(v.shape), -1, axis)


WIDE = False


def mx_kscale(k):
    if not WIDE:
        return np.ones(k)
    levels = np.array([10, -10, 5, -5, 0])
    if k % 512:
        return np.exp2(np.random.permutation(np.resize(levels, k // 32))).repeat(32)
    a = np.empty((k // 512, 16))
    for p in range(k // 512):
        a[p, :8] = np.random.permutation(np.resize(levels, 8))
        for g in range(8):
            far = levels[np.abs(levels - a[p, g]) >= 10]
            a[p, g + 8] = far[np.random.randint(len(far))]
    return np.exp2(a.ravel()).repeat(32)


def f64(x):
    return np.asarray(x).astype(np.float64)


E2M1 = np.array([0.0, 0.5, 1.0, 1.5, 2.0, 3.0, 4.0, 6.0, -0.0, -0.5, -1.0, -1.5, -2.0, -3.0, -4.0, -6.0])


def pack_weight(w, fmt):
    k, n = w.shape
    w = f64(np.asarray(w, np.float32).astype(ml_dtypes.bfloat16)).reshape(k // 32, 32, n)
    amax = np.abs(w).max(1)
    if fmt == "e4m3":
        byte = np.frexp(amax)[1] - 1 + 127 - 7
    else:
        mant, ex = np.frexp(amax / 6.0)
        byte = np.where(mant > 0.5, ex, ex - 1) + 127
    byte = np.clip(np.where(amax > 0, byte, 1), 1, 254)
    scaled = (w * np.exp2(127.0 - byte)[:, None, :]).reshape(k, n).astype(np.float32)
    by_word = np.ascontiguousarray(scaled.reshape(k // 512, 128, 4, n).transpose(0, 1, 3, 2))
    if fmt == "e4m3":
        words = by_word.astype(ml_dtypes.float8_e4m3fn).view(np.uint8)
    else:
        c = by_word.astype(ml_dtypes.float4_e2m1fn).view(np.uint8) & 0xF
        words = (c[..., 0::2] | (c[..., 1::2] << 4)).reshape(k // 512, 128, 2 * n)
    return np.ascontiguousarray(words), np.ascontiguousarray(byte.astype(np.uint8).reshape(k // 512, 16, n))


def unpack_weight(words, scales, fmt):
    g, _, n = scales.shape
    words = np.ascontiguousarray(words).reshape(g, 128, n, -1)
    if fmt == "e4m3":
        vals = words.view(ml_dtypes.float8_e4m3fn).astype(np.float64)
    else:
        nib = np.empty((g, 128, n, 4), np.uint8)
        nib[..., 0::2] = words & 0xF
        nib[..., 1::2] = words >> 4
        vals = E2M1[nib]
    vals = vals * np.repeat(np.exp2(scales.astype(np.float64) - 127.0), 8, axis=1)[..., None]
    return vals.transpose(0, 1, 3, 2).reshape(g * 512, n)


def planes(y):
    n, m = y.shape
    v = y.astype(np.float32).astype(ml_dtypes.bfloat16).astype(np.float64).reshape(n // 32, 32, m)
    top = np.abs(v).max(1)
    byte = np.clip(np.where(top > 0, np.frexp(top)[1] - 1 + 127 - 7, 1), 1, 254)
    codes = (v * np.exp2(127.0 - byte)[:, None, :]).reshape(n, m).astype(np.float32).astype(ml_dtypes.float8_e4m3fn).view(np.uint8)
    words = codes.reshape(n // 512, 128, 4, m).transpose(0, 1, 3, 2)
    return np.ascontiguousarray(words), np.ascontiguousarray(byte.astype(np.uint8).reshape(n // 512, 16, m))


D, K, M, T = 256, 512, 1536, 512


def setup_inputs():
    n = np.random.standard_normal
    s = mx_kscale(K)[:, None]
    p_w0 = pack_weight(n((K, M)) / np.sqrt(K) / s, "e2m1")
    p_w1 = pack_weight(n((K, M)) / np.sqrt(K) / s, "e4m3")
    return {
        "x": (n((K, T + 2 * D)) * s).astype(np.float32),
        "w0_words": p_w0[0],
        "w0_scales": p_w0[1],
        "w1_words": p_w1[0],
        "w1_scales": p_w1[1],
        "w2": (n((K, M)) / np.sqrt(K) / s).astype(np.float32),
        "g": (n((1536, 512))).astype(np.float32),
    }


def reference(x, w0_words, w0_scales, w1_words, w1_scales, w2, g):
    x_ = mxq(f64(x), 0, "e4m3")
    w0_ = unpack_weight(w0_words, w0_scales, "e2m1")
    w1_ = unpack_weight(w1_words, w1_scales, "e4m3")
    w2_ = mxq(f64(w2), 0, "e4m3")
    y = w0_.T @ x_[:, :T] + w1_.T @ x_[:, D:D + T] + w2_.T @ x_[:, 2 * D:]
    out_0 = f64(g) * y
    return (out_0,) + planes(out_0)

@@ -1,0 +1,234 @@
+from contextlib import ExitStack
+
+import concourse.mybir as mybir
+
+D, K, M, T = 256, 512, 1536, 512
+XW = T + 2 * D
+FLOPS = 2 * 3 * K * M * T
+
+F32 = mybir.dt.float32
+BF16 = mybir.dt.bfloat16
+I32 = mybir.dt.int32
+U32 = mybir.dt.uint32
+U8 = mybir.dt.uint8
+FP8X4 = mybir.dt.float8_e4m3fn_x4
+FP4X4 = mybir.dt.float4_e2m1fn_x4
+
+P = 128
+PACK = 4
+CH = P * PACK
+NCH = M // CH
+HALF = T // 2
+W1_ROW = 4
+
+
+def interleave(copy, dst, src):
+    copy(
+        out=dst.rearrange("p (c i) j -> p c j i", i=4),
+        in_=src.rearrange("p j (c i) -> p c j i", i=4),
+    )
+
+
+def tile_mix_dconv_fm_pl_mul_kernel(
+    tc, x, w0_words, w0_scales, w1_words, w1_scales, w2, g, out_0, out_1, out_2
+):
+    nc = tc.nc
+    with ExitStack() as ctx:
+        sb = ctx.enter_context(tc.tile_pool(name="sb", bufs=1))
+        psum = ctx.enter_context(tc.psum_pool(name="psum", bufs=1))
+        ctx.enter_context(tc.manual_schedule())
+
+        w1_raw = sb.tile([P, M], I32, name="w1_raw")
+        w0_raw = sb.tile([P, 2 * M], U8, name="w0_raw")
+        ws_raw = sb.tile([P, M], U8, name="ws_raw")
+        x_raw = sb.tile([P, PACK, XW], F32, name="x_raw")
+        w2_raw = [sb.tile([P, PACK, CH], F32, name="w2_raw%d" % a) for a in range(NCH)]
+        g_sb = [sb.tile([P, PACK, T], F32, name="g_sb%d" % a) for a in range(NCH)]
+
+        def load_scale_rows(src, row0, quad):
+            nc.sync.dma_start(
+                out=ws_raw[32 * quad + row0 : 32 * quad + row0 + 4, :].bitcast(I32),
+                in_=src[0, 4 * quad : 4 * quad + 4, :].bitcast(I32),
+            )
+
+        x_rows = x.rearrange("(p j) t -> p j t", j=PACK)
+        w2_rows = w2.rearrange("(p j) n -> p j n", j=PACK)
+
+        def load_w2(a):
+            nc.sync.dma_start(out=w2_raw[a][:], in_=w2_rows[:, :, a * CH : (a + 1) * CH])
+
+        def load_g(a):
+            nc.sync.dma_start(
+                out=g_sb[a][:], in_=g[a * CH : (a + 1) * CH, :].rearrange("(p r) t -> p r t", r=PACK)
+            )
+
+        nc.vector.memset(ws_raw[:].bitcast(I32), 0)
+        nc.sync.dma_start(out=w1_raw[:], in_=w1_words[0].rearrange("p n i -> p (n i)").bitcast(I32))
+        for quad in range(4):
+            load_scale_rows(w0_scales, 0, quad)
+        nc.sync.dma_start(out=w0_raw[:].bitcast(I32), in_=w0_words[0].bitcast(I32))
+        nc.sync.dma_start(out=x_raw[:, 0:2, :], in_=x_rows[:, 0:2, :])
+        for quad in range(4):
+            load_scale_rows(w1_scales, W1_ROW, quad)
+        nc.sync.dma_start(out=x_raw[:, 2:4, :], in_=x_rows[:, 2:4, :])
+        load_w2(0)
+        load_g(0)
+        load_w2(1)
+        load_w2(2)
+        load_g(1)
+        load_g(2)
+
+        w1_codes = sb.tile([P, M], U32, name="w1_codes", align_bytes=64)
+        w0_codes = sb.tile([P, 2 * M], U8, name="w0_codes", align_bytes=64)
+        ws = sb.tile([P, M], U8, name="ws", align_bytes=64)
+        nc.vector.tensor_copy(
+            out=w1_codes[:].bitcast(I32).rearrange("p (a r m) -> p a m r", a=NCH, r=PACK),
+            in_=w1_raw[:].rearrange("p (a m r) -> p a m r", a=NCH, r=PACK),
+        )
+        nc.vector.tensor_copy(
+            out=w0_codes[:].rearrange("p (a r m b) -> p a m r b", a=NCH, r=PACK, b=2),
+            in_=w0_raw[:].rearrange("p (a m r b) -> p a m r b", a=NCH, r=PACK, b=2),
+        )
+        nc.vector.tensor_copy(
+            out=ws[:].rearrange("p (a r m) -> p a m r", a=NCH, r=PACK),
+            in_=ws_raw[:].rearrange("p (a m r) -> p a m r", a=NCH, r=PACK),
+        )
+
+        x_codes = sb.tile([P, XW], U32, name="x_codes", align_bytes=64)
+        x_scales = sb.tile([P, XW], U8, name="x_scales", align_bytes=64)
+
+        def cast_x(copy, c0, c1):
+            grouped = sb.tile([P, c1 - c0, PACK], BF16, name="x_bf%d" % c0, align_bytes=64)
+            interleave(copy, grouped[:], x_raw[:, :, c0:c1])
+            return grouped
+
+        def quantize(grouped, codes, scales):
+            nc.vector.quantize_mx(
+                out=codes.bitcast(FP8X4), scales=scales, in_=grouped[:].rearrange("p c j -> p (c j)")
+            )
+
+        x_a = cast_x(nc.vector.tensor_copy, 0, 2 * D)
+        x_b = cast_x(nc.scalar.copy, 2 * D, 3 * D)
+        x_c = cast_x(nc.scalar.copy, 3 * D, 4 * D)
+        quantize(x_b, x_codes[:, 2 * D : 3 * D], x_scales[:, 2 * D : 3 * D])
+        quantize(x_a, x_codes[:, 0 : 2 * D], x_scales[:, 0 : 2 * D])
+        quantize(x_c, x_codes[:, 3 * D : 4 * D], x_scales[:, 3 * D : 4 * D])
+
+        w2_codes = [sb.tile([P, CH], U32, name="w2_codes%d" % a, align_bytes=64) for a in range(NCH)]
+        w2_scales = [sb.tile([P, CH], U8, name="w2_scales%d" % a, align_bytes=64) for a in range(NCH)]
+        y_sb = [sb.tile([P, PACK, T], F32, name="y_sb%d" % a) for a in range(NCH)]
+        o_codes = [sb.tile([P, T], U32, name="o_codes%d" % a, align_bytes=64) for a in range(NCH)]
+        o_scales = sb.tile([P, NCH, T], U8, name="o_scales", align_bytes=64)
+
+        def cast_w2(a):
+            grouped = sb.tile([P, CH, PACK], BF16, name="w2_bf%d" % a, align_bytes=64)
+            nc.scalar.copy(
+                out=grouped[:].rearrange("p (r m) j -> p m j r", r=PACK),
+                in_=w2_raw[a][:].rearrange("p j (m r) -> p m j r", r=PACK),
+            )
+            return grouped
+
+        def open_sums(a):
+            banks = []
+            for r in range(PACK):
+                s = PACK * a + r
+                acc = psum.tile([P, T], F32, name="bank%d" % (s % 8))
+                cols = slice(s * P, (s + 1) * P)
+                nc.tensor.matmul_mx(
+                    out=acc[:],
+                    lhsT=w0_codes[:, 2 * s * P : 2 * (s + 1) * P].bitcast(FP4X4),
+                    lhsT_scale=ws[:, cols],
+                    rhs=x_codes[:, 0:T].bitcast(FP8X4),
+                    rhs_scale=x_scales[:, 0:T],
+                    start=True,
+                    stop=False,
+                )
+                nc.tensor.matmul_mx(
+                    out=acc[:],
+                    lhsT=w1_codes[:, cols].bitcast(FP8X4),
+                    lhsT_scale=ws[W1_ROW:P, cols],
+                    rhs=x_codes[:, D : D + T].bitcast(FP8X4),
+                    rhs_scale=x_scales[:, D : D + T],
+                    start=False,
+                    stop=False,
+                )
+                banks.append(acc)
+            return banks
+
+        def close_sums(a, banks):
+            for r in range(PACK):
+                cols = slice(r * P, (r + 1) * P)
+                nc.tensor.matmul_mx(
+                    out=banks[r][:],
+                    lhsT=w2_codes[a][:, cols].bitcast(FP8X4),
+                    lhsT_scale=w2_scales[a][:, cols],
+                    rhs=x_codes[:, 2 * D : 2 * D + T].bitcast(FP8X4),
+                    rhs_scale=x_scales[:, 2 * D : 2 * D + T],
+                    start=False,
+                    stop=True,
+                )
+
+        def gate(a, banks, rows):
+            for r in rows:
+                nc.vector.tensor_tensor(
+                    out=y_sb[a][:, r, :], in0=banks[r][:], in1=g_sb[a][:, r, :], op=mybir.AluOpType.mult
+                )
+
+        def store_y(a):
+            nc.sync.dma_start(
+                out=out_0[a * CH : (a + 1) * CH, :].rearrange("(p r) t -> p r t", r=PACK), in_=y_sb[a][:]
+            )
+
+        def cast_y(copy, a, h):
+            grouped = sb.tile([P, HALF, PACK], BF16, name="y_bf%d_%d" % (a, h), align_bytes=64)
+            interleave(copy, grouped[:], y_sb[a][:, :, h * HALF : (h + 1) * HALF])
+            return grouped
+
+        def quantize_y(a, h, grouped):
+            cols = slice(h * HALF, (h + 1) * HALF)
+            quantize(grouped, o_codes[a][:, cols], o_scales[:, a, cols])
+
+        def store_codes(a):
+            nc.sync.dma_start(
+                out=out_1[a].rearrange("p t i -> p (t i)").bitcast(I32), in_=o_codes[a][:].bitcast(I32)
+            )
+
+        def quantize_w2(a, grouped):
+            quantize(grouped, w2_codes[a][:], w2_scales[a][:])
+
+        all_rows = range(PACK)
+        banks0 = open_sums(0)
+        quantize_w2(0, cast_w2(0))
+        close_sums(0, banks0)
+        banks1 = open_sums(1)
+        w2_bf1 = cast_w2(1)
+        gate(0, banks0, all_rows)
+        store_y(0)
+        banks2 = open_sums(2)
+        y0 = [cast_y(nc.vector.tensor_copy, 0, h) for h in range(2)]
+        quantize_w2(1, w2_bf1)
+        close_sums(1, banks1)
+        for h in range(2):
+            quantize_y(0, h, y0[h])
+        store_codes(0)
+        w2_bf2 = cast_w2(2)
+        gate(1, banks1, [0])
+        quantize_w2(2, w2_bf2)
+        close_sums(2, banks2)
+        gate(1, banks1, [1, 2, 3])
+        store_y(1)
+        y1 = [cast_y(nc.scalar.copy, 1, h) for h in range(2)]
+        gate(2, banks2, all_rows)
+        store_y(2)
+        quantize_y(1, 0, y1[0])
+        y2 = [cast_y(nc.vector.tensor_copy, 2, 0), cast_y(nc.scalar.copy, 2, 1)]
+        quantize_y(1, 1, y1[1])
+        store_codes(1)
+        for h in range(2):
+            quantize_y(2, h, y2[h])
+        store_codes(2)
+        for quad in range(4):
+            nc.scalar.dma_start(
+                out=out_2[:, 4 * quad : 4 * quad + 4, :].rearrange("a r t -> r a t").bitcast(I32),
+                in_=o_scales[32 * quad : 32 * quad + 4, :, :].bitcast(I32),
+            )

@@ -63,14 +63,14 @@ def tile_mix_dconv_fm_pl_mul_kernel(
             )
 
         nc.vector.memset(ws_raw[:].bitcast(I32), 0)
-        nc.sync.dma_start(out=w1_raw[:], in_=w1_words[0].rearrange("p n i -> p (n i)").bitcast(I32))
+        nc.sync.dma_start(out=w0_raw[:].bitcast(I32), in_=w0_words[0].bitcast(I32))
         for quad in range(4):
             load_scale_rows(w0_scales, 0, quad)
-        nc.sync.dma_start(out=w0_raw[:].bitcast(I32), in_=w0_words[0].bitcast(I32))
-        nc.sync.dma_start(out=x_raw[:, 0:2, :], in_=x_rows[:, 0:2, :])
+        nc.sync.dma_start(out=x_raw[:, 0:3, :], in_=x_rows[:, 0:3, :])
         for quad in range(4):
             load_scale_rows(w1_scales, W1_ROW, quad)
-        nc.sync.dma_start(out=x_raw[:, 2:4, :], in_=x_rows[:, 2:4, :])
+        nc.sync.dma_start(out=x_raw[:, 3:4, :], in_=x_rows[:, 3:4, :])
+        nc.sync.dma_start(out=w1_raw[:], in_=w1_words[0].rearrange("p n i -> p (n i)").bitcast(I32))
         load_w2(0)
         load_g(0)
         load_w2(1)
@@ -81,18 +81,18 @@ def tile_mix_dconv_fm_pl_mul_kernel(
         w1_codes = sb.tile([P, M], U32, name="w1_codes", align_bytes=64)
         w0_codes = sb.tile([P, 2 * M], U8, name="w0_codes", align_bytes=64)
         ws = sb.tile([P, M], U8, name="ws", align_bytes=64)
-        nc.vector.tensor_copy(
-            out=w1_codes[:].bitcast(I32).rearrange("p (a r m) -> p a m r", a=NCH, r=PACK),
-            in_=w1_raw[:].rearrange("p (a m r) -> p a m r", a=NCH, r=PACK),
-        )
-        nc.vector.tensor_copy(
-            out=w0_codes[:].rearrange("p (a r m b) -> p a m r b", a=NCH, r=PACK, b=2),
-            in_=w0_raw[:].rearrange("p (a m r b) -> p a m r b", a=NCH, r=PACK, b=2),
-        )
-        nc.vector.tensor_copy(
-            out=ws[:].rearrange("p (a r m) -> p a m r", a=NCH, r=PACK),
-            in_=ws_raw[:].rearrange("p (a m r) -> p a m r", a=NCH, r=PACK),
-        )
+        for a in range(NCH):
+            byte_cols = slice(2 * a * CH, 2 * (a + 1) * CH)
+            nc.vector.tensor_copy(
+                out=w0_codes[:, byte_cols].rearrange("p (r m b) -> p r m b", r=PACK, b=2),
+                in_=w0_raw[:, byte_cols].rearrange("p (m r b) -> p r m b", r=PACK, b=2),
+            )
+        for a in range(NCH):
+            cols = slice(a * CH, (a + 1) * CH)
+            nc.vector.tensor_copy(
+                out=ws[:, cols].rearrange("p (r m) -> p r m", r=PACK),
+                in_=ws_raw[:, cols].rearrange("p (m r) -> p r m", r=PACK),
+            )
 
         x_codes = sb.tile([P, XW], U32, name="x_codes", align_bytes=64)
         x_scales = sb.tile([P, XW], U8, name="x_scales", align_bytes=64)
@@ -113,6 +113,12 @@ def tile_mix_dconv_fm_pl_mul_kernel(
         quantize(x_b, x_codes[:, 2 * D : 3 * D], x_scales[:, 2 * D : 3 * D])
         quantize(x_a, x_codes[:, 0 : 2 * D], x_scales[:, 0 : 2 * D])
         quantize(x_c, x_codes[:, 3 * D : 4 * D], x_scales[:, 3 * D : 4 * D])
+        for a in range(NCH):
+            cols = slice(a * CH, (a + 1) * CH)
+            nc.vector.tensor_copy(
+                out=w1_codes[:, cols].bitcast(I32).rearrange("p (r m) -> p m r", r=PACK),
+                in_=w1_raw[:, cols].rearrange("p (m r) -> p m r", r=PACK),
+            )
 
         w2_codes = [sb.tile([P, CH], U32, name="w2_codes%d" % a, align_bytes=64) for a in range(NCH)]
         w2_scales = [sb.tile([P, CH], U8, name="w2_scales%d" % a, align_bytes=64) for a in range(NCH)]
@@ -120,17 +126,18 @@ def tile_mix_dconv_fm_pl_mul_kernel(
         o_codes = [sb.tile([P, T], U32, name="o_codes%d" % a, align_bytes=64) for a in range(NCH)]
         o_scales = sb.tile([P, NCH, T], U8, name="o_scales", align_bytes=64)
 
-        def cast_w2(a):
-            grouped = sb.tile([P, CH, PACK], BF16, name="w2_bf%d" % a, align_bytes=64)
-            nc.scalar.copy(
-                out=grouped[:].rearrange("p (r m) j -> p m j r", r=PACK),
-                in_=w2_raw[a][:].rearrange("p j (m r) -> p m j r", r=PACK),
-            )
-            return grouped
+        w2_bf = [sb.tile([P, CH, PACK], BF16, name="w2_bf%d" % a, align_bytes=64) for a in range(NCH)]
 
-        def open_sums(a):
-            banks = []
-            for r in range(PACK):
+        def cast_w2(copy, a, m0, m1):
+            copy(
+                out=w2_bf[a][:].rearrange("p (r m) j -> p m j r", r=PACK)[:, m0:m1, :, :],
+                in_=w2_raw[a][:].rearrange("p j (m r) -> p m j r", r=PACK)[:, m0:m1, :, :],
+            )
+
+        banks = {}
+
+        def open_sums(a, rows):
+            for r in rows:
                 s = PACK * a + r
                 acc = psum.tile([P, T], F32, name="bank%d" % (s % 8))
                 cols = slice(s * P, (s + 1) * P)
@@ -143,8 +150,14 @@ def tile_mix_dconv_fm_pl_mul_kernel(
                     start=True,
                     stop=False,
                 )
+                banks[a, r] = acc
+
+        def add_w1(a, rows):
+            for r in rows:
+                s = PACK * a + r
+                cols = slice(s * P, (s + 1) * P)
                 nc.tensor.matmul_mx(
-                    out=acc[:],
+                    out=banks[a, r][:],
                     lhsT=w1_codes[:, cols].bitcast(FP8X4),
                     lhsT_scale=ws[W1_ROW:P, cols],
                     rhs=x_codes[:, D : D + T].bitcast(FP8X4),
@@ -152,14 +165,12 @@ def tile_mix_dconv_fm_pl_mul_kernel(
                     start=False,
                     stop=False,
                 )
-                banks.append(acc)
-            return banks
 
-        def close_sums(a, banks):
-            for r in range(PACK):
+        def close_sums(a, rows):
+            for r in rows:
                 cols = slice(r * P, (r + 1) * P)
                 nc.tensor.matmul_mx(
-                    out=banks[r][:],
+                    out=banks[a, r][:],
                     lhsT=w2_codes[a][:, cols].bitcast(FP8X4),
                     lhsT_scale=w2_scales[a][:, cols],
                     rhs=x_codes[:, 2 * D : 2 * D + T].bitcast(FP8X4),
@@ -168,10 +179,10 @@ def tile_mix_dconv_fm_pl_mul_kernel(
                     stop=True,
                 )
 
-        def gate(a, banks, rows):
+        def gate(a, rows):
             for r in rows:
                 nc.vector.tensor_tensor(
-                    out=y_sb[a][:, r, :], in0=banks[r][:], in1=g_sb[a][:, r, :], op=mybir.AluOpType.mult
+                    out=y_sb[a][:, r, :], in0=banks[a, r][:], in1=g_sb[a][:, r, :], op=mybir.AluOpType.mult
                 )
 
         def store_y(a):
@@ -193,36 +204,42 @@ def tile_mix_dconv_fm_pl_mul_kernel(
                 out=out_1[a].rearrange("p t i -> p (t i)").bitcast(I32), in_=o_codes[a][:].bitcast(I32)
             )
 
-        def quantize_w2(a, grouped):
-            quantize(grouped, w2_codes[a][:], w2_scales[a][:])
+        def quantize_w2(a):
+            quantize(w2_bf[a], w2_codes[a][:], w2_scales[a][:])
 
         all_rows = range(PACK)
-        banks0 = open_sums(0)
-        quantize_w2(0, cast_w2(0))
-        close_sums(0, banks0)
-        banks1 = open_sums(1)
-        w2_bf1 = cast_w2(1)
-        gate(0, banks0, all_rows)
+        on_vector, on_scalar = nc.vector.tensor_copy, nc.scalar.copy
+        open_sums(0, all_rows)
+        add_w1(0, all_rows)
+        cast_w2(on_vector, 0, 0, 84)
+        cast_w2(on_scalar, 0, 84, P)
+        quantize_w2(0)
+        close_sums(0, all_rows)
+        open_sums(1, all_rows)
+        add_w1(1, all_rows)
+        cast_w2(on_scalar, 1, 0, P)
+        gate(0, all_rows)
         store_y(0)
-        banks2 = open_sums(2)
-        y0 = [cast_y(nc.vector.tensor_copy, 0, h) for h in range(2)]
-        quantize_w2(1, w2_bf1)
-        close_sums(1, banks1)
+        open_sums(2, all_rows)
+        add_w1(2, all_rows)
+        y0 = [cast_y(on_vector, 0, h) for h in range(2)]
         for h in range(2):
             quantize_y(0, h, y0[h])
         store_codes(0)
-        w2_bf2 = cast_w2(2)
-        gate(1, banks1, [0])
-        quantize_w2(2, w2_bf2)
-        close_sums(2, banks2)
-        gate(1, banks1, [1, 2, 3])
+        quantize_w2(1)
+        close_sums(1, all_rows)
+        cast_w2(on_vector, 2, 0, 64)
+        cast_w2(on_scalar, 2, 64, P)
+        quantize_w2(2)
+        close_sums(2, all_rows)
+        gate(1, all_rows)
         store_y(1)
-        y1 = [cast_y(nc.scalar.copy, 1, h) for h in range(2)]
-        gate(2, banks2, all_rows)
+        y1 = [cast_y(on_scalar, 1, h) for h in range(2)]
+        gate(2, all_rows)
         store_y(2)
-        quantize_y(1, 0, y1[0])
-        y2 = [cast_y(nc.vector.tensor_copy, 2, 0), cast_y(nc.scalar.copy, 2, 1)]
-        quantize_y(1, 1, y1[1])
+        y2 = [cast_y(on_vector, 2, 0), cast_y(on_scalar, 2, 1)]
+        for h in range(2):
+            quantize_y(1, h, y1[h])
         store_codes(1)
         for h in range(2):
             quantize_y(2, h, y2[h])

@@ -45,11 +45,12 @@ def tile_mix_dconv_fm_pl_mul_kernel(
         w2_raw = [sb.tile([P, PACK, CH], F32, name="w2_raw%d" % a) for a in range(NCH)]
         g_sb = [sb.tile([P, PACK, T], F32, name="g_sb%d" % a) for a in range(NCH)]
 
-        def load_scale_rows(src, row0, quad):
-            nc.sync.dma_start(
-                out=ws_raw[32 * quad + row0 : 32 * quad + row0 + 4, :].bitcast(I32),
-                in_=src[0, 4 * quad : 4 * quad + 4, :].bitcast(I32),
-            )
+        def load_scale_rows(r):
+            for src, row0 in ((w0_scales, 0), (w1_scales, W1_ROW)):
+                nc.sync.dma_start(
+                    out=ws_raw[row0 + r : P : 32, :].bitcast(I32),
+                    in_=src[0, r:16:4, :].bitcast(I32),
+                )
 
         x_rows = x.rearrange("(p j) t -> p j t", j=PACK)
         w2_rows = w2.rearrange("(p j) n -> p j n", j=PACK)
@@ -64,11 +65,11 @@ def tile_mix_dconv_fm_pl_mul_kernel(
 
         nc.vector.memset(ws_raw[:].bitcast(I32), 0)
         nc.sync.dma_start(out=w0_raw[:].bitcast(I32), in_=w0_words[0].bitcast(I32))
-        for quad in range(4):
-            load_scale_rows(w0_scales, 0, quad)
+        for r in range(2):
+            load_scale_rows(r)
         nc.sync.dma_start(out=x_raw[:, 0:3, :], in_=x_rows[:, 0:3, :])
-        for quad in range(4):
-            load_scale_rows(w1_scales, W1_ROW, quad)
+        for r in range(2, 4):
+            load_scale_rows(r)
         nc.sync.dma_start(out=x_raw[:, 3:4, :], in_=x_rows[:, 3:4, :])
         nc.sync.dma_start(out=w1_raw[:], in_=w1_words[0].rearrange("p n i -> p (n i)").bitcast(I32))
         load_w2(0)
@@ -244,8 +245,8 @@ def tile_mix_dconv_fm_pl_mul_kernel(
         for h in range(2):
             quantize_y(2, h, y2[h])
         store_codes(2)
-        for quad in range(4):
+        for r in range(4):
             nc.scalar.dma_start(
-                out=out_2[:, 4 * quad : 4 * quad + 4, :].rearrange("a r t -> r a t").bitcast(I32),
-                in_=o_scales[32 * quad : 32 * quad + 4, :, :].bitcast(I32),
+                out=out_2[:, r:16:4, :].rearrange("a q t -> q a t").bitcast(I32),
+                in_=o_scales[r:P:32, :, :].bitcast(I32),
             )

@@ -10,6 +10,7 @@ F32 = mybir.dt.float32
 BF16 = mybir.dt.bfloat16
 I32 = mybir.dt.int32
 U32 = mybir.dt.uint32
+U16 = mybir.dt.uint16
 U8 = mybir.dt.uint8
 FP8X4 = mybir.dt.float8_e4m3fn_x4
 FP4X4 = mybir.dt.float4_e2m1fn_x4
@@ -20,6 +21,7 @@ CH = P * PACK
 NCH = M // CH
 HALF = T // 2
 W1_ROW = 4
+OUT_ROW = 8
 
 
 def interleave(copy, dst, src):
@@ -38,12 +40,12 @@ def tile_mix_dconv_fm_pl_mul_kernel(
         psum = ctx.enter_context(tc.psum_pool(name="psum", bufs=1))
         ctx.enter_context(tc.manual_schedule())
 
-        w1_raw = sb.tile([P, M], I32, name="w1_raw")
-        w0_raw = sb.tile([P, 2 * M], U8, name="w0_raw")
-        ws_raw = sb.tile([P, M], U8, name="ws_raw")
-        x_raw = sb.tile([P, PACK, XW], F32, name="x_raw")
-        w2_raw = [sb.tile([P, PACK, CH], F32, name="w2_raw%d" % a) for a in range(NCH)]
-        g_sb = [sb.tile([P, PACK, T], F32, name="g_sb%d" % a) for a in range(NCH)]
+        w1_raw = sb.tile([P, M], I32, name="w1_raw", align_bytes=256)
+        w0_raw = sb.tile([P, 2 * M], U8, name="w0_raw", align_bytes=256)
+        ws_raw = sb.tile([P, M], U8, name="ws_raw", align_bytes=256)
+        x_raw = sb.tile([P, PACK, XW], F32, name="x_raw", align_bytes=256)
+        w2_raw = [sb.tile([P, PACK, CH], F32, name="w2_raw%d" % a, align_bytes=256) for a in range(NCH)]
+        g_sb = [sb.tile([P, PACK, T], F32, name="g_sb%d" % a, align_bytes=256) for a in range(NCH)]
 
         def load_scale_rows(r):
             for src, row0 in ((w0_scales, 0), (w1_scales, W1_ROW)):
@@ -67,10 +69,9 @@ def tile_mix_dconv_fm_pl_mul_kernel(
         nc.sync.dma_start(out=w0_raw[:].bitcast(I32), in_=w0_words[0].bitcast(I32))
         for r in range(2):
             load_scale_rows(r)
-        nc.sync.dma_start(out=x_raw[:, 0:3, :], in_=x_rows[:, 0:3, :])
+        nc.sync.dma_start(out=x_raw[:], in_=x_rows)
         for r in range(2, 4):
             load_scale_rows(r)
-        nc.sync.dma_start(out=x_raw[:, 3:4, :], in_=x_rows[:, 3:4, :])
         nc.sync.dma_start(out=w1_raw[:], in_=w1_words[0].rearrange("p n i -> p (n i)").bitcast(I32))
         load_w2(0)
         load_g(0)
@@ -79,27 +80,28 @@ def tile_mix_dconv_fm_pl_mul_kernel(
         load_g(1)
         load_g(2)
 
-        w1_codes = sb.tile([P, M], U32, name="w1_codes", align_bytes=64)
-        w0_codes = sb.tile([P, 2 * M], U8, name="w0_codes", align_bytes=64)
-        ws = sb.tile([P, M], U8, name="ws", align_bytes=64)
+        w1_codes = sb.tile([P, M], U32, name="w1_codes", align_bytes=256)
+        w0_codes = sb.tile([P, 2 * M], U8, name="w0_codes", align_bytes=256)
+        ws = sb.tile([P, M], U8, name="ws", align_bytes=256)
         for a in range(NCH):
             byte_cols = slice(2 * a * CH, 2 * (a + 1) * CH)
             nc.vector.tensor_copy(
-                out=w0_codes[:, byte_cols].rearrange("p (r m b) -> p r m b", r=PACK, b=2),
-                in_=w0_raw[:, byte_cols].rearrange("p (m r b) -> p r m b", r=PACK, b=2),
+                out=w0_codes[:, byte_cols].bitcast(U16).rearrange("p (r c i) -> p c r i", r=PACK, i=8),
+                in_=w0_raw[:, byte_cols].bitcast(U16).rearrange("p (c i r) -> p c r i", r=PACK, i=8),
             )
-        for a in range(NCH):
+
+        def deal_scales(a):
             cols = slice(a * CH, (a + 1) * CH)
             nc.vector.tensor_copy(
                 out=ws[:, cols].rearrange("p (r m) -> p r m", r=PACK),
                 in_=ws_raw[:, cols].rearrange("p (m r) -> p r m", r=PACK),
             )
 
-        x_codes = sb.tile([P, XW], U32, name="x_codes", align_bytes=64)
-        x_scales = sb.tile([P, XW], U8, name="x_scales", align_bytes=64)
+        x_codes = sb.tile([P, XW], U32, name="x_codes", align_bytes=256)
+        x_scales = sb.tile([P, XW], U8, name="x_scales", align_bytes=256)
 
         def cast_x(copy, c0, c1):
-            grouped = sb.tile([P, c1 - c0, PACK], BF16, name="x_bf%d" % c0, align_bytes=64)
+            grouped = sb.tile([P, c1 - c0, PACK], BF16, name="x_bf%d" % c0, align_bytes=256)
             interleave(copy, grouped[:], x_raw[:, :, c0:c1])
             return grouped
 
@@ -108,26 +110,24 @@ def tile_mix_dconv_fm_pl_mul_kernel(
                 out=codes.bitcast(FP8X4), scales=scales, in_=grouped[:].rearrange("p c j -> p (c j)")
             )
 
-        x_a = cast_x(nc.vector.tensor_copy, 0, 2 * D)
-        x_b = cast_x(nc.scalar.copy, 2 * D, 3 * D)
-        x_c = cast_x(nc.scalar.copy, 3 * D, 4 * D)
-        quantize(x_b, x_codes[:, 2 * D : 3 * D], x_scales[:, 2 * D : 3 * D])
-        quantize(x_a, x_codes[:, 0 : 2 * D], x_scales[:, 0 : 2 * D])
-        quantize(x_c, x_codes[:, 3 * D : 4 * D], x_scales[:, 3 * D : 4 * D])
-        for a in range(NCH):
+        def quantize_x(q, grouped):
+            cols = slice(q * D, (q + 1) * D)
+            quantize(grouped, x_codes[:, cols], x_scales[:, cols])
+
+        def deal_w1(a):
             cols = slice(a * CH, (a + 1) * CH)
             nc.vector.tensor_copy(
                 out=w1_codes[:, cols].bitcast(I32).rearrange("p (r m) -> p m r", r=PACK),
                 in_=w1_raw[:, cols].rearrange("p (m r) -> p m r", r=PACK),
             )
 
-        w2_codes = [sb.tile([P, CH], U32, name="w2_codes%d" % a, align_bytes=64) for a in range(NCH)]
-        w2_scales = [sb.tile([P, CH], U8, name="w2_scales%d" % a, align_bytes=64) for a in range(NCH)]
-        y_sb = [sb.tile([P, PACK, T], F32, name="y_sb%d" % a) for a in range(NCH)]
-        o_codes = [sb.tile([P, T], U32, name="o_codes%d" % a, align_bytes=64) for a in range(NCH)]
-        o_scales = sb.tile([P, NCH, T], U8, name="o_scales", align_bytes=64)
+        w2_codes = [sb.tile([P, CH], U32, name="w2_codes%d" % a, align_bytes=256) for a in range(NCH)]
+        w2_scales = [sb.tile([P, CH], U8, name="w2_scales%d" % a, align_bytes=256) for a in range(NCH)]
+        y_sb = [sb.tile([P, PACK, T], F32, name="y_sb%d" % a, align_bytes=256) for a in range(NCH)]
+        o_codes = sb.tile([P, NCH, T], U32, name="o_codes", align_bytes=256)
+        o_scales = sb.tile([P, NCH, T], U8, name="o_scales", align_bytes=256)
 
-        w2_bf = [sb.tile([P, CH, PACK], BF16, name="w2_bf%d" % a, align_bytes=64) for a in range(NCH)]
+        w2_bf = [sb.tile([P, CH, PACK], BF16, name="w2_bf%d" % a, align_bytes=256) for a in range(NCH)]
 
         def cast_w2(copy, a, m0, m1):
             copy(
@@ -192,17 +192,18 @@ def tile_mix_dconv_fm_pl_mul_kernel(
             )
 
         def cast_y(copy, a, h):
-            grouped = sb.tile([P, HALF, PACK], BF16, name="y_bf%d_%d" % (a, h), align_bytes=64)
+            grouped = sb.tile([P, HALF, PACK], BF16, name="y_bf%d_%d" % (a, h), align_bytes=256)
             interleave(copy, grouped[:], y_sb[a][:, :, h * HALF : (h + 1) * HALF])
             return grouped
 
         def quantize_y(a, h, grouped):
             cols = slice(h * HALF, (h + 1) * HALF)
-            quantize(grouped, o_codes[a][:, cols], o_scales[:, a, cols])
+            quantize(grouped, o_codes[:, a, cols], o_scales[OUT_ROW:P, a, cols])
 
-        def store_codes(a):
+        def store_codes(a0, a1):
             nc.sync.dma_start(
-                out=out_1[a].rearrange("p t i -> p (t i)").bitcast(I32), in_=o_codes[a][:].bitcast(I32)
+                out=out_1[a0:a1].rearrange("a p t i -> p a (t i)").bitcast(I32),
+                in_=o_codes[:, a0:a1, :].bitcast(I32),
             )
 
         def quantize_w2(a):
@@ -210,30 +211,48 @@ def tile_mix_dconv_fm_pl_mul_kernel(
 
         all_rows = range(PACK)
         on_vector, on_scalar = nc.vector.tensor_copy, nc.scalar.copy
+        x0 = cast_x(on_vector, 0, D)
+        x1 = cast_x(on_scalar, D, 2 * D)
+        x3 = cast_x(on_scalar, 3 * D, 4 * D)
+        deal_scales(0)
+        quantize_x(0, x0)
+        quantize_x(1, x1)
         open_sums(0, all_rows)
+        x2 = cast_x(on_vector, 2 * D, 3 * D)
+        deal_w1(0)
+        quantize_x(2, x2)
         add_w1(0, all_rows)
+        quantize_x(3, x3)
+        deal_scales(1)
+        open_sums(1, range(3))
         cast_w2(on_vector, 0, 0, 84)
         cast_w2(on_scalar, 0, 84, P)
+        deal_w1(1)
         quantize_w2(0)
         close_sums(0, all_rows)
-        open_sums(1, all_rows)
+        open_sums(1, range(3, 4))
         add_w1(1, all_rows)
-        cast_w2(on_scalar, 1, 0, P)
+        deal_scales(2)
+        deal_w1(2)
         gate(0, all_rows)
         store_y(0)
         open_sums(2, all_rows)
-        add_w1(2, all_rows)
-        y0 = [cast_y(on_vector, 0, h) for h in range(2)]
-        for h in range(2):
-            quantize_y(0, h, y0[h])
-        store_codes(0)
+        cast_w2(on_scalar, 1, 76, P)
+        cast_w2(on_vector, 1, 0, 76)
+        y0 = [cast_y(on_scalar, 0, 0)]
         quantize_w2(1)
         close_sums(1, all_rows)
-        cast_w2(on_vector, 2, 0, 64)
-        cast_w2(on_scalar, 2, 64, P)
+        add_w1(2, all_rows)
+        cast_w2(on_vector, 2, 0, 92)
+        cast_w2(on_scalar, 2, 92, P)
+        y0.append(cast_y(on_scalar, 0, 1))
+        quantize_y(0, 0, y0[0])
         quantize_w2(2)
         close_sums(2, all_rows)
-        gate(1, all_rows)
+        gate(1, range(1))
+        quantize_y(0, 1, y0[1])
+        store_codes(0, 1)
+        gate(1, range(1, 4))
         store_y(1)
         y1 = [cast_y(on_scalar, 1, h) for h in range(2)]
         gate(2, all_rows)
@@ -241,12 +260,11 @@ def tile_mix_dconv_fm_pl_mul_kernel(
         y2 = [cast_y(on_vector, 2, 0), cast_y(on_scalar, 2, 1)]
         for h in range(2):
             quantize_y(1, h, y1[h])
-        store_codes(1)
         for h in range(2):
             quantize_y(2, h, y2[h])
-        store_codes(2)
+        store_codes(1, 3)
         for r in range(4):
             nc.scalar.dma_start(
                 out=out_2[:, r:16:4, :].rearrange("a q t -> q a t").bitcast(I32),
-                in_=o_scales[r:P:32, :, :].bitcast(I32),
+                in_=o_scales[OUT_ROW + r : P : 32, :, :].bitcast(I32),
             )

@@ -180,10 +180,13 @@ def tile_mix_dconv_fm_pl_mul_kernel(
                     stop=True,
                 )
 
-        def gate(a, rows):
+        def gate(a, rows, t0=0, t1=T):
             for r in rows:
                 nc.vector.tensor_tensor(
-                    out=y_sb[a][:, r, :], in0=banks[a, r][:], in1=g_sb[a][:, r, :], op=mybir.AluOpType.mult
+                    out=y_sb[a][:, r, t0:t1],
+                    in0=banks[a, r][:, t0:t1],
+                    in1=g_sb[a][:, r, t0:t1],
+                    op=mybir.AluOpType.mult,
                 )
 
         def store_y(a):
@@ -191,14 +194,17 @@ def tile_mix_dconv_fm_pl_mul_kernel(
                 out=out_0[a * CH : (a + 1) * CH, :].rearrange("(p r) t -> p r t", r=PACK), in_=y_sb[a][:]
             )
 
-        def cast_y(copy, a, h):
-            grouped = sb.tile([P, HALF, PACK], BF16, name="y_bf%d_%d" % (a, h), align_bytes=256)
-            interleave(copy, grouped[:], y_sb[a][:, :, h * HALF : (h + 1) * HALF])
-            return grouped
+        y_bf = [
+            [sb.tile([P, HALF, PACK], BF16, name="y_bf%d_%d" % (a, h), align_bytes=256) for h in range(2)]
+            for a in range(NCH)
+        ]
 
-        def quantize_y(a, h, grouped):
+        def cast_y(copy, a, h, c0=0, c1=HALF):
+            interleave(copy, y_bf[a][h][:, c0:c1, :], y_sb[a][:, :, h * HALF + c0 : h * HALF + c1])
+
+        def quantize_y(a, h):
             cols = slice(h * HALF, (h + 1) * HALF)
-            quantize(grouped, o_codes[:, a, cols], o_scales[OUT_ROW:P, a, cols])
+            quantize(y_bf[a][h], o_codes[:, a, cols], o_scales[OUT_ROW:P, a, cols])
 
         def store_codes(a0, a1):
             nc.sync.dma_start(
@@ -234,34 +240,39 @@ def tile_mix_dconv_fm_pl_mul_kernel(
         add_w1(1, all_rows)
         deal_scales(2)
         deal_w1(2)
-        gate(0, all_rows)
+        gate(0, all_rows, 0, HALF)
+        gate(0, all_rows, HALF, T)
         store_y(0)
         open_sums(2, all_rows)
-        cast_w2(on_scalar, 1, 76, P)
-        cast_w2(on_vector, 1, 0, 76)
-        y0 = [cast_y(on_scalar, 0, 0)]
+        cast_y(on_scalar, 0, 0)
+        cast_w2(on_scalar, 1, 92, P)
+        cast_w2(on_vector, 1, 0, 92)
+        cast_y(on_scalar, 0, 1)
+        quantize_y(0, 0)
         quantize_w2(1)
         close_sums(1, all_rows)
         add_w1(2, all_rows)
-        cast_w2(on_vector, 2, 0, 92)
-        cast_w2(on_scalar, 2, 92, P)
-        y0.append(cast_y(on_scalar, 0, 1))
-        quantize_y(0, 0, y0[0])
+        cast_w2(on_vector, 2, 0, 84)
+        cast_w2(on_scalar, 2, 84, P)
+        quantize_y(0, 1)
+        store_codes(0, 1)
         quantize_w2(2)
         close_sums(2, all_rows)
-        gate(1, range(1))
-        quantize_y(0, 1, y0[1])
-        store_codes(0, 1)
-        gate(1, range(1, 4))
+        gate(1, all_rows, 0, HALF)
+        cast_y(on_scalar, 1, 0)
+        gate(1, all_rows, HALF, T)
         store_y(1)
-        y1 = [cast_y(on_scalar, 1, h) for h in range(2)]
-        gate(2, all_rows)
+        cast_y(on_scalar, 1, 1)
+        gate(2, all_rows, 0, HALF)
+        cast_y(on_scalar, 2, 0)
+        gate(2, all_rows, HALF, T)
         store_y(2)
-        y2 = [cast_y(on_vector, 2, 0), cast_y(on_scalar, 2, 1)]
-        for h in range(2):
-            quantize_y(1, h, y1[h])
-        for h in range(2):
-            quantize_y(2, h, y2[h])
+        quantize_y(1, 0)
+        cast_y(on_vector, 2, 1, 0, 160)
+        cast_y(on_scalar, 2, 1, 160, HALF)
+        quantize_y(1, 1)
+        quantize_y(2, 0)
+        quantize_y(2, 1)
         store_codes(1, 3)
         for r in range(4):
             nc.scalar.dma_start(

@@ -44,7 +44,9 @@ def tile_mix_dconv_fm_pl_mul_kernel(
         w0_raw = sb.tile([P, 2 * M], U8, name="w0_raw", align_bytes=256)
         ws_raw = sb.tile([P, M], U8, name="ws_raw", align_bytes=256)
         x_raw = sb.tile([P, PACK, XW], F32, name="x_raw", align_bytes=256)
-        w2_raw = [sb.tile([P, PACK, CH], F32, name="w2_raw%d" % a, align_bytes=256) for a in range(NCH)]
+        w2_first = sb.tile([P, PACK, 2 * CH], F32, name="w2_first", align_bytes=256)
+        w2_last = sb.tile([P, PACK, CH], F32, name="w2_last", align_bytes=256)
+        w2_raw = [w2_first[:, :, 0:CH], w2_first[:, :, CH : 2 * CH], w2_last[:]]
         g_sb = [sb.tile([P, PACK, T], F32, name="g_sb%d" % a, align_bytes=256) for a in range(NCH)]
 
         def load_scale_rows(r):
@@ -56,9 +58,6 @@ def tile_mix_dconv_fm_pl_mul_kernel(
 
         x_rows = x.rearrange("(p j) t -> p j t", j=PACK)
         w2_rows = w2.rearrange("(p j) n -> p j n", j=PACK)
-
-        def load_w2(a):
-            nc.sync.dma_start(out=w2_raw[a][:], in_=w2_rows[:, :, a * CH : (a + 1) * CH])
 
         def load_g(a):
             nc.sync.dma_start(
@@ -73,10 +72,9 @@ def tile_mix_dconv_fm_pl_mul_kernel(
         for r in range(2, 4):
             load_scale_rows(r)
         nc.sync.dma_start(out=w1_raw[:], in_=w1_words[0].rearrange("p n i -> p (n i)").bitcast(I32))
-        load_w2(0)
+        nc.sync.dma_start(out=w2_first[:], in_=w2_rows[:, :, 0 : 2 * CH])
         load_g(0)
-        load_w2(1)
-        load_w2(2)
+        nc.sync.dma_start(out=w2_last[:], in_=w2_rows[:, :, 2 * CH : M])
         load_g(1)
         load_g(2)
 
@@ -132,7 +130,7 @@ def tile_mix_dconv_fm_pl_mul_kernel(
         def cast_w2(copy, a, m0, m1):
             copy(
                 out=w2_bf[a][:].rearrange("p (r m) j -> p m j r", r=PACK)[:, m0:m1, :, :],
-                in_=w2_raw[a][:].rearrange("p j (m r) -> p m j r", r=PACK)[:, m0:m1, :, :],
+                in_=w2_raw[a].rearrange("p j (m r) -> p m j r", r=PACK)[:, m0:m1, :, :],
             )
 
         banks = {}
@@ -229,37 +227,35 @@ def tile_mix_dconv_fm_pl_mul_kernel(
         quantize_x(2, x2)
         add_w1(0, all_rows)
         quantize_x(3, x3)
-        deal_scales(1)
-        open_sums(1, range(3))
+        for a in range(1, NCH):
+            deal_scales(a)
+            deal_w1(a)
+        open_sums(1, all_rows)
+        add_w1(1, all_rows)
         cast_w2(on_vector, 0, 0, 84)
         cast_w2(on_scalar, 0, 84, P)
-        deal_w1(1)
+        cast_w2(on_vector, 1, 0, 44)
+        cast_w2(on_scalar, 1, 44, P)
         quantize_w2(0)
         close_sums(0, all_rows)
-        open_sums(1, range(3, 4))
-        add_w1(1, all_rows)
-        deal_scales(2)
-        deal_w1(2)
         gate(0, all_rows, 0, HALF)
+        cast_y(on_scalar, 0, 0)
+        quantize_w2(1)
+        close_sums(1, all_rows)
         gate(0, all_rows, HALF, T)
         store_y(0)
         open_sums(2, all_rows)
-        cast_y(on_scalar, 0, 0)
-        cast_w2(on_scalar, 1, 92, P)
-        cast_w2(on_vector, 1, 0, 92)
-        cast_y(on_scalar, 0, 1)
-        quantize_y(0, 0)
-        quantize_w2(1)
-        close_sums(1, all_rows)
         add_w1(2, all_rows)
         cast_w2(on_vector, 2, 0, 84)
         cast_w2(on_scalar, 2, 84, P)
-        quantize_y(0, 1)
-        store_codes(0, 1)
+        cast_y(on_scalar, 0, 1)
+        quantize_y(0, 0)
         quantize_w2(2)
         close_sums(2, all_rows)
         gate(1, all_rows, 0, HALF)
         cast_y(on_scalar, 1, 0)
+        quantize_y(0, 1)
+        store_codes(0, 1)
         gate(1, all_rows, HALF, T)
         store_y(1)
         cast_y(on_scalar, 1, 1)

@@ -14,14 +14,17 @@ U16 = mybir.dt.uint16
 U8 = mybir.dt.uint8
 FP8X4 = mybir.dt.float8_e4m3fn_x4
 FP4X4 = mybir.dt.float4_e2m1fn_x4
+MULT = mybir.AluOpType.mult
 
 P = 128
 PACK = 4
 CH = P * PACK
 NCH = M // CH
 HALF = T // 2
+BANKS = 8
 W1_ROW = 4
 OUT_ROW = 8
+ALIGN = 256
 
 
 def interleave(copy, dst, src):
@@ -39,53 +42,50 @@ def tile_mix_dconv_fm_pl_mul_kernel(
         sb = ctx.enter_context(tc.tile_pool(name="sb", bufs=1))
         psum = ctx.enter_context(tc.psum_pool(name="psum", bufs=1))
         ctx.enter_context(tc.manual_schedule())
+        on_vector, on_scalar = nc.vector.tensor_copy, nc.scalar.copy
 
-        w1_raw = sb.tile([P, M], I32, name="w1_raw", align_bytes=256)
-        w0_raw = sb.tile([P, 2 * M], U8, name="w0_raw", align_bytes=256)
-        ws_raw = sb.tile([P, M], U8, name="ws_raw", align_bytes=256)
-        x_raw = sb.tile([P, PACK, XW], F32, name="x_raw", align_bytes=256)
-        w2_first = sb.tile([P, PACK, 2 * CH], F32, name="w2_first", align_bytes=256)
-        w2_last = sb.tile([P, PACK, CH], F32, name="w2_last", align_bytes=256)
+        def tile(name, shape, dtype):
+            return sb.tile(shape, dtype, name=name, align_bytes=ALIGN)
+
+        w0_raw, w0_codes = tile("w0_raw", [P, 2 * M], U8), tile("w0_codes", [P, 2 * M], U8)
+        w1_raw, w1_codes = tile("w1_raw", [P, M], I32), tile("w1_codes", [P, M], U32)
+        ws_raw, ws = tile("ws_raw", [P, M], U8), tile("ws", [P, M], U8)
+        x_raw = tile("x_raw", [P, PACK, XW], F32)
+        x_bf = [tile("x_bf%d" % q, [P, D, PACK], BF16) for q in range(XW // D)]
+        x_codes, x_scales = tile("x_codes", [P, XW], U32), tile("x_scales", [P, XW], U8)
+        w2_first, w2_last = tile("w2_first", [P, PACK, 2 * CH], F32), tile("w2_last", [P, PACK, CH], F32)
         w2_raw = [w2_first[:, :, 0:CH], w2_first[:, :, CH : 2 * CH], w2_last[:]]
-        g_sb = [sb.tile([P, PACK, T], F32, name="g_sb%d" % a, align_bytes=256) for a in range(NCH)]
+        w2_bf = [tile("w2_bf%d" % a, [P, CH, PACK], BF16) for a in range(NCH)]
+        w2_codes = [tile("w2_codes%d" % a, [P, CH], U32) for a in range(NCH)]
+        w2_scales = [tile("w2_scales%d" % a, [P, CH], U8) for a in range(NCH)]
+        g_sb = [tile("g_sb%d" % a, [P, PACK, T], F32) for a in range(NCH)]
+        y_first, y_last = tile("y_first", [P, 2, PACK, T], F32), tile("y_last", [P, PACK, T], F32)
+        y_sb = [y_first[:, 0], y_first[:, 1], y_last[:]]
+        y_bf = [[tile("y_bf%d_%d" % (a, h), [P, HALF, PACK], BF16) for h in range(2)] for a in range(NCH)]
+        o_codes, o_scales = tile("o_codes", [P, NCH, T], U32), tile("o_scales", [P, NCH, T], U8)
 
         def load_scale_rows(r):
             for src, row0 in ((w0_scales, 0), (w1_scales, W1_ROW)):
                 nc.sync.dma_start(
-                    out=ws_raw[row0 + r : P : 32, :].bitcast(I32),
-                    in_=src[0, r:16:4, :].bitcast(I32),
+                    out=ws_raw[row0 + r : P : 32, :].bitcast(I32), in_=src[0, r:16:4, :].bitcast(I32)
                 )
 
-        x_rows = x.rearrange("(p j) t -> p j t", j=PACK)
-        w2_rows = w2.rearrange("(p j) n -> p j n", j=PACK)
-
         def load_g(a):
-            nc.sync.dma_start(
-                out=g_sb[a][:], in_=g[a * CH : (a + 1) * CH, :].rearrange("(p r) t -> p r t", r=PACK)
+            rows = g[a * CH : (a + 1) * CH, :]
+            nc.sync.dma_start(out=g_sb[a][:], in_=rows.rearrange("(p r) t -> p r t", r=PACK))
+
+        def deal_w0(a):
+            cols = slice(2 * a * CH, 2 * (a + 1) * CH)
+            nc.vector.tensor_copy(
+                out=w0_codes[:, cols].bitcast(U16).rearrange("p (r c i) -> p c r i", r=PACK, i=8),
+                in_=w0_raw[:, cols].bitcast(U16).rearrange("p (c i r) -> p c r i", r=PACK, i=8),
             )
 
-        nc.vector.memset(ws_raw[:].bitcast(I32), 0)
-        nc.sync.dma_start(out=w0_raw[:].bitcast(I32), in_=w0_words[0].bitcast(I32))
-        for r in range(2):
-            load_scale_rows(r)
-        nc.sync.dma_start(out=x_raw[:], in_=x_rows)
-        for r in range(2, 4):
-            load_scale_rows(r)
-        nc.sync.dma_start(out=w1_raw[:], in_=w1_words[0].rearrange("p n i -> p (n i)").bitcast(I32))
-        nc.sync.dma_start(out=w2_first[:], in_=w2_rows[:, :, 0 : 2 * CH])
-        load_g(0)
-        nc.sync.dma_start(out=w2_last[:], in_=w2_rows[:, :, 2 * CH : M])
-        load_g(1)
-        load_g(2)
-
-        w1_codes = sb.tile([P, M], U32, name="w1_codes", align_bytes=256)
-        w0_codes = sb.tile([P, 2 * M], U8, name="w0_codes", align_bytes=256)
-        ws = sb.tile([P, M], U8, name="ws", align_bytes=256)
-        for a in range(NCH):
-            byte_cols = slice(2 * a * CH, 2 * (a + 1) * CH)
+        def deal_w1(a):
+            cols = slice(a * CH, (a + 1) * CH)
             nc.vector.tensor_copy(
-                out=w0_codes[:, byte_cols].bitcast(U16).rearrange("p (r c i) -> p c r i", r=PACK, i=8),
-                in_=w0_raw[:, byte_cols].bitcast(U16).rearrange("p (c i r) -> p c r i", r=PACK, i=8),
+                out=w1_codes[:, cols].bitcast(I32).rearrange("p (r m) -> p m r", r=PACK),
+                in_=w1_raw[:, cols].rearrange("p (m r) -> p m r", r=PACK),
             )
 
         def deal_scales(a):
@@ -95,37 +95,17 @@ def tile_mix_dconv_fm_pl_mul_kernel(
                 in_=ws_raw[:, cols].rearrange("p (m r) -> p r m", r=PACK),
             )
 
-        x_codes = sb.tile([P, XW], U32, name="x_codes", align_bytes=256)
-        x_scales = sb.tile([P, XW], U8, name="x_scales", align_bytes=256)
-
-        def cast_x(copy, c0, c1):
-            grouped = sb.tile([P, c1 - c0, PACK], BF16, name="x_bf%d" % c0, align_bytes=256)
-            interleave(copy, grouped[:], x_raw[:, :, c0:c1])
-            return grouped
-
         def quantize(grouped, codes, scales):
             nc.vector.quantize_mx(
                 out=codes.bitcast(FP8X4), scales=scales, in_=grouped[:].rearrange("p c j -> p (c j)")
             )
 
-        def quantize_x(q, grouped):
+        def cast_x(copy, q):
+            interleave(copy, x_bf[q][:], x_raw[:, :, q * D : (q + 1) * D])
+
+        def quantize_x(q):
             cols = slice(q * D, (q + 1) * D)
-            quantize(grouped, x_codes[:, cols], x_scales[:, cols])
-
-        def deal_w1(a):
-            cols = slice(a * CH, (a + 1) * CH)
-            nc.vector.tensor_copy(
-                out=w1_codes[:, cols].bitcast(I32).rearrange("p (r m) -> p m r", r=PACK),
-                in_=w1_raw[:, cols].rearrange("p (m r) -> p m r", r=PACK),
-            )
-
-        w2_codes = [sb.tile([P, CH], U32, name="w2_codes%d" % a, align_bytes=256) for a in range(NCH)]
-        w2_scales = [sb.tile([P, CH], U8, name="w2_scales%d" % a, align_bytes=256) for a in range(NCH)]
-        y_sb = [sb.tile([P, PACK, T], F32, name="y_sb%d" % a, align_bytes=256) for a in range(NCH)]
-        o_codes = sb.tile([P, NCH, T], U32, name="o_codes", align_bytes=256)
-        o_scales = sb.tile([P, NCH, T], U8, name="o_scales", align_bytes=256)
-
-        w2_bf = [sb.tile([P, CH, PACK], BF16, name="w2_bf%d" % a, align_bytes=256) for a in range(NCH)]
+            quantize(x_bf[q], x_codes[:, cols], x_scales[:, cols])
 
         def cast_w2(copy, a, m0, m1):
             copy(
@@ -133,69 +113,49 @@ def tile_mix_dconv_fm_pl_mul_kernel(
                 in_=w2_raw[a].rearrange("p j (m r) -> p m j r", r=PACK)[:, m0:m1, :, :],
             )
 
+        def quantize_w2(a):
+            quantize(w2_bf[a], w2_codes[a][:], w2_scales[a][:])
+
         banks = {}
 
-        def open_sums(a, rows):
+        def tap(a, r, codes, scales, t0, start=False, stop=False):
+            nc.tensor.matmul_mx(
+                out=banks[a, r][:],
+                lhsT=codes,
+                lhsT_scale=scales,
+                rhs=x_codes[:, t0 : t0 + T].bitcast(FP8X4),
+                rhs_scale=x_scales[:, t0 : t0 + T],
+                start=start,
+                stop=stop,
+            )
+
+        def open_with_w1(a, rows):
             for r in rows:
                 s = PACK * a + r
-                acc = psum.tile([P, T], F32, name="bank%d" % (s % 8))
+                banks[a, r] = psum.tile([P, T], F32, name="bank%d" % (s % BANKS))
                 cols = slice(s * P, (s + 1) * P)
-                nc.tensor.matmul_mx(
-                    out=acc[:],
-                    lhsT=w0_codes[:, 2 * s * P : 2 * (s + 1) * P].bitcast(FP4X4),
-                    lhsT_scale=ws[:, cols],
-                    rhs=x_codes[:, 0:T].bitcast(FP8X4),
-                    rhs_scale=x_scales[:, 0:T],
-                    start=True,
-                    stop=False,
-                )
-                banks[a, r] = acc
+                tap(a, r, w1_codes[:, cols].bitcast(FP8X4), ws[W1_ROW:P, cols], D, start=True)
 
-        def add_w1(a, rows):
+        def add_w0(a, rows):
             for r in rows:
                 s = PACK * a + r
-                cols = slice(s * P, (s + 1) * P)
-                nc.tensor.matmul_mx(
-                    out=banks[a, r][:],
-                    lhsT=w1_codes[:, cols].bitcast(FP8X4),
-                    lhsT_scale=ws[W1_ROW:P, cols],
-                    rhs=x_codes[:, D : D + T].bitcast(FP8X4),
-                    rhs_scale=x_scales[:, D : D + T],
-                    start=False,
-                    stop=False,
-                )
+                codes = w0_codes[:, 2 * s * P : 2 * (s + 1) * P]
+                tap(a, r, codes.bitcast(FP4X4), ws[:, s * P : (s + 1) * P], 0)
 
-        def close_sums(a, rows):
+        def close_with_w2(a, rows):
             for r in rows:
                 cols = slice(r * P, (r + 1) * P)
-                nc.tensor.matmul_mx(
-                    out=banks[a, r][:],
-                    lhsT=w2_codes[a][:, cols].bitcast(FP8X4),
-                    lhsT_scale=w2_scales[a][:, cols],
-                    rhs=x_codes[:, 2 * D : 2 * D + T].bitcast(FP8X4),
-                    rhs_scale=x_scales[:, 2 * D : 2 * D + T],
-                    start=False,
-                    stop=True,
-                )
+                tap(a, r, w2_codes[a][:, cols].bitcast(FP8X4), w2_scales[a][:, cols], 2 * D, stop=True)
 
         def gate(a, rows, t0=0, t1=T):
             for r in rows:
                 nc.vector.tensor_tensor(
-                    out=y_sb[a][:, r, t0:t1],
-                    in0=banks[a, r][:, t0:t1],
-                    in1=g_sb[a][:, r, t0:t1],
-                    op=mybir.AluOpType.mult,
+                    out=y_sb[a][:, r, t0:t1], in0=banks[a, r][:, t0:t1], in1=g_sb[a][:, r, t0:t1], op=MULT
                 )
 
-        def store_y(a):
-            nc.sync.dma_start(
-                out=out_0[a * CH : (a + 1) * CH, :].rearrange("(p r) t -> p r t", r=PACK), in_=y_sb[a][:]
-            )
-
-        y_bf = [
-            [sb.tile([P, HALF, PACK], BF16, name="y_bf%d_%d" % (a, h), align_bytes=256) for h in range(2)]
-            for a in range(NCH)
-        ]
+        def gate_aside(a, r):
+            nc.scalar.copy(out=y_sb[a][:, r, :], in_=banks[a, r][:])
+            nc.gpsimd.tensor_tensor(out=y_sb[a][:, r, :], in0=y_sb[a][:, r, :], in1=g_sb[a][:, r, :], op=MULT)
 
         def cast_y(copy, a, h, c0=0, c1=HALF):
             interleave(copy, y_bf[a][h][:, c0:c1, :], y_sb[a][:, :, h * HALF + c0 : h * HALF + c1])
@@ -210,65 +170,83 @@ def tile_mix_dconv_fm_pl_mul_kernel(
                 in_=o_codes[:, a0:a1, :].bitcast(I32),
             )
 
-        def quantize_w2(a):
-            quantize(w2_bf[a], w2_codes[a][:], w2_scales[a][:])
+        every = range(PACK)
+        aside_first = (3, 0, 1, 2)
+        w2_rows = w2.rearrange("(p j) n -> p j n", j=PACK)
+        nc.vector.memset(ws_raw[:].bitcast(I32), 0)
+        nc.sync.dma_start(out=w1_raw[:], in_=w1_words[0].rearrange("p n i -> p (n i)").bitcast(I32))
+        for r in range(2):
+            load_scale_rows(r)
+        nc.sync.dma_start(out=x_raw[:], in_=x.rearrange("(p j) t -> p j t", j=PACK))
+        for r in range(2, 4):
+            load_scale_rows(r)
+        nc.sync.dma_start(out=w0_raw[:].bitcast(I32), in_=w0_words[0].bitcast(I32))
+        nc.sync.dma_start(out=w2_first[:], in_=w2_rows[:, :, 0 : 2 * CH])
+        load_g(0)
+        load_g(1)
+        nc.sync.dma_start(out=w2_last[:], in_=w2_rows[:, :, 2 * CH : M])
+        load_g(2)
 
-        all_rows = range(PACK)
-        on_vector, on_scalar = nc.vector.tensor_copy, nc.scalar.copy
-        x0 = cast_x(on_vector, 0, D)
-        x1 = cast_x(on_scalar, D, 2 * D)
-        x3 = cast_x(on_scalar, 3 * D, 4 * D)
-        deal_scales(0)
-        quantize_x(0, x0)
-        quantize_x(1, x1)
-        open_sums(0, all_rows)
-        x2 = cast_x(on_vector, 2 * D, 3 * D)
-        deal_w1(0)
-        quantize_x(2, x2)
-        add_w1(0, all_rows)
-        quantize_x(3, x3)
-        for a in range(1, NCH):
-            deal_scales(a)
+        for a in range(NCH):
             deal_w1(a)
-        open_sums(1, all_rows)
-        add_w1(1, all_rows)
+        cast_x(on_vector, 1)
+        cast_x(on_scalar, 2)
+        cast_x(on_scalar, 3)
+        deal_scales(0)
+        quantize_x(1)
+        quantize_x(2)
+        open_with_w1(0, every)
+        cast_x(on_vector, 0)
+        deal_scales(1)
+        open_with_w1(1, every)
+        quantize_x(0)
+        deal_w0(0)
+        add_w0(0, every)
+        quantize_x(3)
+        deal_w0(1)
+        deal_w0(2)
+        add_w0(1, every)
+        deal_scales(2)
         cast_w2(on_vector, 0, 0, 84)
         cast_w2(on_scalar, 0, 84, P)
-        cast_w2(on_vector, 1, 0, 44)
-        cast_w2(on_scalar, 1, 44, P)
+        cast_w2(on_vector, 1, 0, 60)
+        cast_w2(on_scalar, 1, 60, P)
         quantize_w2(0)
-        close_sums(0, all_rows)
-        gate(0, all_rows, 0, HALF)
-        cast_y(on_scalar, 0, 0)
+        close_with_w2(0, aside_first)
         quantize_w2(1)
-        close_sums(1, all_rows)
-        gate(0, all_rows, HALF, T)
-        store_y(0)
-        open_sums(2, all_rows)
-        add_w1(2, all_rows)
+        close_with_w2(1, aside_first)
+        gate(0, range(3))
+        gate_aside(0, 3)
+        gate_aside(1, 3)
+        cast_y(on_scalar, 0, 0)
+        gate(1, range(3))
+        nc.sync.dma_start(
+            out=out_0[0 : 2 * CH, :].rearrange("(a p r) t -> p a (r t)", a=2, r=PACK),
+            in_=y_first[:].rearrange("p a r t -> p a (r t)"),
+        )
+        open_with_w1(2, every)
+        add_w0(2, every)
         cast_w2(on_vector, 2, 0, 84)
         cast_w2(on_scalar, 2, 84, P)
         cast_y(on_scalar, 0, 1)
+        cast_y(on_scalar, 1, 0)
+        cast_y(on_scalar, 1, 1)
         quantize_y(0, 0)
         quantize_w2(2)
-        close_sums(2, all_rows)
-        gate(1, all_rows, 0, HALF)
-        cast_y(on_scalar, 1, 0)
+        close_with_w2(2, every)
+        gate(2, every, 0, HALF)
+        cast_y(on_scalar, 2, 0)
         quantize_y(0, 1)
         store_codes(0, 1)
-        gate(1, all_rows, HALF, T)
-        store_y(1)
-        cast_y(on_scalar, 1, 1)
-        gate(2, all_rows, 0, HALF)
-        cast_y(on_scalar, 2, 0)
-        gate(2, all_rows, HALF, T)
-        store_y(2)
+        gate(2, every, HALF, T)
+        nc.sync.dma_start(
+            out=out_0[2 * CH : M, :].rearrange("(p r) t -> p r t", r=PACK), in_=y_last[:]
+        )
         quantize_y(1, 0)
-        cast_y(on_vector, 2, 1, 0, 160)
-        cast_y(on_scalar, 2, 1, 160, HALF)
+        cast_y(on_vector, 2, 1)
         quantize_y(1, 1)
-        quantize_y(2, 0)
         quantize_y(2, 1)
+        quantize_y(2, 0)
         store_codes(1, 3)
         for r in range(4):
             nc.scalar.dma_start(

@@ -53,14 +53,12 @@ def tile_mix_dconv_fm_pl_mul_kernel(
         x_raw = tile("x_raw", [P, PACK, XW], F32)
         x_bf = [tile("x_bf%d" % q, [P, D, PACK], BF16) for q in range(XW // D)]
         x_codes, x_scales = tile("x_codes", [P, XW], U32), tile("x_scales", [P, XW], U8)
-        w2_first, w2_last = tile("w2_first", [P, PACK, 2 * CH], F32), tile("w2_last", [P, PACK, CH], F32)
-        w2_raw = [w2_first[:, :, 0:CH], w2_first[:, :, CH : 2 * CH], w2_last[:]]
+        w2_raw = [tile("w2_raw%d" % a, [P, PACK, CH], F32) for a in range(NCH)]
         w2_bf = [tile("w2_bf%d" % a, [P, CH, PACK], BF16) for a in range(NCH)]
         w2_codes = [tile("w2_codes%d" % a, [P, CH], U32) for a in range(NCH)]
         w2_scales = [tile("w2_scales%d" % a, [P, CH], U8) for a in range(NCH)]
         g_sb = [tile("g_sb%d" % a, [P, PACK, T], F32) for a in range(NCH)]
-        y_first, y_last = tile("y_first", [P, 2, PACK, T], F32), tile("y_last", [P, PACK, T], F32)
-        y_sb = [y_first[:, 0], y_first[:, 1], y_last[:]]
+        y_sb = [tile("y_sb%d" % a, [P, PACK, T], F32) for a in range(NCH)]
         y_bf = [[tile("y_bf%d_%d" % (a, h), [P, HALF, PACK], BF16) for h in range(2)] for a in range(NCH)]
         o_codes, o_scales = tile("o_codes", [P, NCH, T], U32), tile("o_scales", [P, NCH, T], U8)
 
@@ -69,6 +67,10 @@ def tile_mix_dconv_fm_pl_mul_kernel(
                 nc.sync.dma_start(
                     out=ws_raw[row0 + r : P : 32, :].bitcast(I32), in_=src[0, r:16:4, :].bitcast(I32)
                 )
+
+        def load_w2(a):
+            rows = w2.rearrange("(p j) n -> p j n", j=PACK)
+            nc.sync.dma_start(out=w2_raw[a][:], in_=rows[:, :, a * CH : (a + 1) * CH])
 
         def load_g(a):
             rows = g[a * CH : (a + 1) * CH, :]
@@ -110,7 +112,7 @@ def tile_mix_dconv_fm_pl_mul_kernel(
         def cast_w2(copy, a, m0, m1):
             copy(
                 out=w2_bf[a][:].rearrange("p (r m) j -> p m j r", r=PACK)[:, m0:m1, :, :],
-                in_=w2_raw[a].rearrange("p j (m r) -> p m j r", r=PACK)[:, m0:m1, :, :],
+                in_=w2_raw[a][:].rearrange("p j (m r) -> p m j r", r=PACK)[:, m0:m1, :, :],
             )
 
         def quantize_w2(a):
@@ -153,8 +155,10 @@ def tile_mix_dconv_fm_pl_mul_kernel(
                     out=y_sb[a][:, r, t0:t1], in0=banks[a, r][:, t0:t1], in1=g_sb[a][:, r, t0:t1], op=MULT
                 )
 
-        def gate_aside(a, r):
+        def park(a, r):
             nc.scalar.copy(out=y_sb[a][:, r, :], in_=banks[a, r][:])
+
+        def gate_parked(a, r):
             nc.gpsimd.tensor_tensor(out=y_sb[a][:, r, :], in0=y_sb[a][:, r, :], in1=g_sb[a][:, r, :], op=MULT)
 
         def cast_y(copy, a, h, c0=0, c1=HALF):
@@ -164,6 +168,10 @@ def tile_mix_dconv_fm_pl_mul_kernel(
             cols = slice(h * HALF, (h + 1) * HALF)
             quantize(y_bf[a][h], o_codes[:, a, cols], o_scales[OUT_ROW:P, a, cols])
 
+        def store_y(a):
+            rows = out_0[a * CH : (a + 1) * CH, :]
+            nc.sync.dma_start(out=rows.rearrange("(p r) t -> p r t", r=PACK), in_=y_sb[a][:])
+
         def store_codes(a0, a1):
             nc.sync.dma_start(
                 out=out_1[a0:a1].rearrange("a p t i -> p a (t i)").bitcast(I32),
@@ -171,8 +179,6 @@ def tile_mix_dconv_fm_pl_mul_kernel(
             )
 
         every = range(PACK)
-        aside_first = (3, 0, 1, 2)
-        w2_rows = w2.rearrange("(p j) n -> p j n", j=PACK)
         nc.vector.memset(ws_raw[:].bitcast(I32), 0)
         nc.sync.dma_start(out=w1_raw[:], in_=w1_words[0].rearrange("p n i -> p (n i)").bitcast(I32))
         for r in range(2):
@@ -181,10 +187,11 @@ def tile_mix_dconv_fm_pl_mul_kernel(
         for r in range(2, 4):
             load_scale_rows(r)
         nc.sync.dma_start(out=w0_raw[:].bitcast(I32), in_=w0_words[0].bitcast(I32))
-        nc.sync.dma_start(out=w2_first[:], in_=w2_rows[:, :, 0 : 2 * CH])
+        load_w2(0)
         load_g(0)
+        load_w2(1)
+        load_w2(2)
         load_g(1)
-        nc.sync.dma_start(out=w2_last[:], in_=w2_rows[:, :, 2 * CH : M])
         load_g(2)
 
         for a in range(NCH):
@@ -197,51 +204,49 @@ def tile_mix_dconv_fm_pl_mul_kernel(
         quantize_x(2)
         open_with_w1(0, every)
         cast_x(on_vector, 0)
-        deal_scales(1)
-        open_with_w1(1, every)
-        quantize_x(0)
         deal_w0(0)
+        quantize_x(0)
         add_w0(0, every)
         quantize_x(3)
-        deal_w0(1)
-        deal_w0(2)
-        add_w0(1, every)
-        deal_scales(2)
         cast_w2(on_vector, 0, 0, 84)
         cast_w2(on_scalar, 0, 84, P)
-        cast_w2(on_vector, 1, 0, 60)
-        cast_w2(on_scalar, 1, 60, P)
+        deal_scales(1)
         quantize_w2(0)
-        close_with_w2(0, aside_first)
-        quantize_w2(1)
-        close_with_w2(1, aside_first)
-        gate(0, range(3))
-        gate_aside(0, 3)
-        gate_aside(1, 3)
+        close_with_w2(0, every)
+        open_with_w1(1, every)
+        deal_w0(1)
+        add_w0(1, every)
+        deal_scales(2)
+        deal_w0(2)
+        gate(0, every, 0, HALF)
         cast_y(on_scalar, 0, 0)
-        gate(1, range(3))
-        nc.sync.dma_start(
-            out=out_0[0 : 2 * CH, :].rearrange("(a p r) t -> p a (r t)", a=2, r=PACK),
-            in_=y_first[:].rearrange("p a r t -> p a (r t)"),
-        )
-        open_with_w1(2, every)
-        add_w0(2, every)
-        cast_w2(on_vector, 2, 0, 84)
-        cast_w2(on_scalar, 2, 84, P)
+        gate(0, every, HALF, T)
+        store_y(0)
         cast_y(on_scalar, 0, 1)
-        cast_y(on_scalar, 1, 0)
-        cast_y(on_scalar, 1, 1)
+        open_with_w1(2, every)
+        cast_w2(on_vector, 1, 0, P)
         quantize_y(0, 0)
-        quantize_w2(2)
-        close_with_w2(2, every)
-        gate(2, every, 0, HALF)
-        cast_y(on_scalar, 2, 0)
+        quantize_w2(1)
+        add_w0(2, range(2))
+        close_with_w2(1, every)
+        add_w0(2, range(2, 4))
+        cast_w2(on_scalar, 2, 44, P)
+        cast_w2(on_vector, 2, 0, 44)
         quantize_y(0, 1)
         store_codes(0, 1)
-        gate(2, every, HALF, T)
-        nc.sync.dma_start(
-            out=out_0[2 * CH : M, :].rearrange("(p r) t -> p r t", r=PACK), in_=y_last[:]
-        )
+        quantize_w2(2)
+        close_with_w2(2, (3, 0, 1, 2))
+        park(2, 3)
+        gate_parked(2, 3)
+        gate(1, every, 0, HALF)
+        cast_y(on_scalar, 1, 0)
+        gate(1, every, HALF, T)
+        store_y(1)
+        cast_y(on_scalar, 1, 1)
+        gate(2, range(3), 0, HALF)
+        cast_y(on_scalar, 2, 0)
+        gate(2, range(3), HALF, T)
+        store_y(2)
         quantize_y(1, 0)
         cast_y(on_vector, 2, 1)
         quantize_y(1, 1)

@@ -173,7 +173,7 @@ def tile_mix_dconv_fm_pl_mul_kernel(
             nc.sync.dma_start(out=rows.rearrange("(p r) t -> p r t", r=PACK), in_=y_sb[a][:])
 
         def store_codes(a0, a1):
-            nc.sync.dma_start(
+            nc.scalar.dma_start(
                 out=out_1[a0:a1].rearrange("a p t i -> p a (t i)").bitcast(I32),
                 in_=o_codes[:, a0:a1, :].bitcast(I32),
             )
@@ -233,10 +233,10 @@ def tile_mix_dconv_fm_pl_mul_kernel(
         cast_w2(on_scalar, 2, 44, P)
         cast_w2(on_vector, 2, 0, 44)
         quantize_y(0, 1)
-        store_codes(0, 1)
         quantize_w2(2)
         close_with_w2(2, (3, 0, 1, 2))
         park(2, 3)
+        store_codes(0, 1)
         gate_parked(2, 3)
         gate(1, every, 0, HALF)
         cast_y(on_scalar, 1, 0)

@@ -168,9 +168,9 @@ def tile_mix_dconv_fm_pl_mul_kernel(
             cols = slice(h * HALF, (h + 1) * HALF)
             quantize(y_bf[a][h], o_codes[:, a, cols], o_scales[OUT_ROW:P, a, cols])
 
-        def store_y(a):
+        def store_y(queue, a):
             rows = out_0[a * CH : (a + 1) * CH, :]
-            nc.sync.dma_start(out=rows.rearrange("(p r) t -> p r t", r=PACK), in_=y_sb[a][:])
+            queue.dma_start(out=rows.rearrange("(p r) t -> p r t", r=PACK), in_=y_sb[a][:])
 
         def store_codes(a0, a1):
             nc.scalar.dma_start(
@@ -221,7 +221,7 @@ def tile_mix_dconv_fm_pl_mul_kernel(
         gate(0, every, 0, HALF)
         cast_y(on_scalar, 0, 0)
         gate(0, every, HALF, T)
-        store_y(0)
+        store_y(nc.sync, 0)
         cast_y(on_scalar, 0, 1)
         open_with_w1(2, every)
         cast_w2(on_vector, 1, 0, P)
@@ -241,12 +241,12 @@ def tile_mix_dconv_fm_pl_mul_kernel(
         gate(1, every, 0, HALF)
         cast_y(on_scalar, 1, 0)
         gate(1, every, HALF, T)
-        store_y(1)
+        store_y(nc.scalar, 1)
         cast_y(on_scalar, 1, 1)
         gate(2, range(3), 0, HALF)
         cast_y(on_scalar, 2, 0)
         gate(2, range(3), HALF, T)
-        store_y(2)
+        store_y(nc.sync, 2)
         quantize_y(1, 0)
         cast_y(on_vector, 2, 1)
         quantize_y(1, 1)
@@ -254,7 +254,7 @@ def tile_mix_dconv_fm_pl_mul_kernel(
         quantize_y(2, 0)
         store_codes(1, 3)
         for r in range(4):
-            nc.scalar.dma_start(
+            nc.sync.dma_start(
                 out=out_2[:, r:16:4, :].rearrange("a q t -> q a t").bitcast(I32),
                 in_=o_scales[OUT_ROW + r : P : 32, :, :].bitcast(I32),
             )

@@ -59,7 +59,7 @@ def tile_mix_dconv_fm_pl_mul_kernel(
         w2_scales = [tile("w2_scales%d" % a, [P, CH], U8) for a in range(NCH)]
         g_sb = [tile("g_sb%d" % a, [P, PACK, T], F32) for a in range(NCH)]
         y_sb = [tile("y_sb%d" % a, [P, PACK, T], F32) for a in range(NCH)]
-        y_bf = [[tile("y_bf%d_%d" % (a, h), [P, HALF, PACK], BF16) for h in range(2)] for a in range(NCH)]
+        y_bf = [tile("y_bf%d" % a, [P, T, PACK], BF16) for a in range(NCH)]
         o_codes, o_scales = tile("o_codes", [P, NCH, T], U32), tile("o_scales", [P, NCH, T], U8)
 
         def load_scale_rows(r):
@@ -76,11 +76,11 @@ def tile_mix_dconv_fm_pl_mul_kernel(
             rows = g[a * CH : (a + 1) * CH, :]
             nc.sync.dma_start(out=g_sb[a][:], in_=rows.rearrange("(p r) t -> p r t", r=PACK))
 
-        def deal_w0(a):
-            cols = slice(2 * a * CH, 2 * (a + 1) * CH)
+        def deal_w0(a0, a1):
+            cols = slice(2 * a0 * CH, 2 * a1 * CH)
             nc.vector.tensor_copy(
-                out=w0_codes[:, cols].bitcast(U16).rearrange("p (r c i) -> p c r i", r=PACK, i=8),
-                in_=w0_raw[:, cols].bitcast(U16).rearrange("p (c i r) -> p c r i", r=PACK, i=8),
+                out=w0_codes[:, cols].bitcast(U16).rearrange("p (a r c i) -> p a c r i", r=PACK, c=16, i=8),
+                in_=w0_raw[:, cols].bitcast(U16).rearrange("p (a c i r) -> p a c r i", r=PACK, c=16, i=8),
             )
 
         def deal_w1(a):
@@ -90,16 +90,16 @@ def tile_mix_dconv_fm_pl_mul_kernel(
                 in_=w1_raw[:, cols].rearrange("p (m r) -> p m r", r=PACK),
             )
 
-        def deal_scales(a):
-            cols = slice(a * CH, (a + 1) * CH)
+        def deal_scales(a0, a1):
+            cols = slice(a0 * CH, a1 * CH)
             nc.vector.tensor_copy(
-                out=ws[:, cols].rearrange("p (r m) -> p r m", r=PACK),
-                in_=ws_raw[:, cols].rearrange("p (m r) -> p r m", r=PACK),
+                out=ws[:, cols].rearrange("p (a r m) -> p a r m", r=PACK, m=P),
+                in_=ws_raw[:, cols].rearrange("p (a m r) -> p a r m", r=PACK, m=P),
             )
 
         def quantize(grouped, codes, scales):
             nc.vector.quantize_mx(
-                out=codes.bitcast(FP8X4), scales=scales, in_=grouped[:].rearrange("p c j -> p (c j)")
+                out=codes.bitcast(FP8X4), scales=scales, in_=grouped.rearrange("p c j -> p (c j)")
             )
 
         def cast_x(copy, q):
@@ -107,7 +107,7 @@ def tile_mix_dconv_fm_pl_mul_kernel(
 
         def quantize_x(q):
             cols = slice(q * D, (q + 1) * D)
-            quantize(x_bf[q], x_codes[:, cols], x_scales[:, cols])
+            quantize(x_bf[q][:], x_codes[:, cols], x_scales[:, cols])
 
         def cast_w2(copy, a, m0, m1):
             copy(
@@ -115,8 +115,9 @@ def tile_mix_dconv_fm_pl_mul_kernel(
                 in_=w2_raw[a][:].rearrange("p j (m r) -> p m j r", r=PACK)[:, m0:m1, :, :],
             )
 
-        def quantize_w2(a):
-            quantize(w2_bf[a], w2_codes[a][:], w2_scales[a][:])
+        def quantize_w2(a, c0=0, c1=CH):
+            cols = slice(c0, c1)
+            quantize(w2_bf[a][:, cols, :], w2_codes[a][:, cols], w2_scales[a][:, cols])
 
         banks = {}
 
@@ -158,15 +159,16 @@ def tile_mix_dconv_fm_pl_mul_kernel(
         def park(a, r):
             nc.scalar.copy(out=y_sb[a][:, r, :], in_=banks[a, r][:])
 
-        def gate_parked(a, r):
-            nc.gpsimd.tensor_tensor(out=y_sb[a][:, r, :], in0=y_sb[a][:, r, :], in1=g_sb[a][:, r, :], op=MULT)
+        def gate_parked(a, r, t0=0, t1=T):
+            nc.gpsimd.tensor_tensor(
+                out=y_sb[a][:, r, t0:t1], in0=y_sb[a][:, r, t0:t1], in1=g_sb[a][:, r, t0:t1], op=MULT
+            )
 
-        def cast_y(copy, a, h, c0=0, c1=HALF):
-            interleave(copy, y_bf[a][h][:, c0:c1, :], y_sb[a][:, :, h * HALF + c0 : h * HALF + c1])
+        def cast_y(copy, a, t0=0, t1=T):
+            interleave(copy, y_bf[a][:, t0:t1, :], y_sb[a][:, :, t0:t1])
 
-        def quantize_y(a, h):
-            cols = slice(h * HALF, (h + 1) * HALF)
-            quantize(y_bf[a][h], o_codes[:, a, cols], o_scales[OUT_ROW:P, a, cols])
+        def quantize_y(a, t0=0, t1=T):
+            quantize(y_bf[a][:, t0:t1, :], o_codes[:, a, t0:t1], o_scales[OUT_ROW:P, a, t0:t1])
 
         def store_y(queue, a):
             rows = out_0[a * CH : (a + 1) * CH, :]
@@ -199,59 +201,54 @@ def tile_mix_dconv_fm_pl_mul_kernel(
         cast_x(on_vector, 1)
         cast_x(on_scalar, 2)
         cast_x(on_scalar, 3)
-        deal_scales(0)
+        deal_scales(0, 1)
         quantize_x(1)
         quantize_x(2)
         open_with_w1(0, every)
         cast_x(on_vector, 0)
-        deal_w0(0)
+        deal_w0(0, 1)
         quantize_x(0)
         add_w0(0, every)
         quantize_x(3)
         cast_w2(on_vector, 0, 0, 84)
         cast_w2(on_scalar, 0, 84, P)
-        deal_scales(1)
-        quantize_w2(0)
-        close_with_w2(0, every)
+        deal_scales(1, 3)
+        quantize_w2(0, 0, CH // 2)
+        quantize_w2(0, CH // 2, CH)
+        close_with_w2(0, (0, 1, 3, 2))
+        deal_w0(1, 3)
         open_with_w1(1, every)
-        deal_w0(1)
         add_w0(1, every)
-        deal_scales(2)
-        deal_w0(2)
-        gate(0, every, 0, HALF)
-        cast_y(on_scalar, 0, 0)
-        gate(0, every, HALF, T)
+        park(0, 3)
+        gate_parked(0, 3)
+        gate(0, range(3))
         store_y(nc.sync, 0)
-        cast_y(on_scalar, 0, 1)
         open_with_w1(2, every)
-        cast_w2(on_vector, 1, 0, P)
-        quantize_y(0, 0)
+        cast_w2(on_scalar, 1, 72, P)
+        cast_w2(on_vector, 1, 0, 72)
+        cast_y(on_scalar, 0, 0, HALF)
+        cast_y(on_scalar, 0, HALF, T)
         quantize_w2(1)
         add_w0(2, range(2))
         close_with_w2(1, every)
         add_w0(2, range(2, 4))
-        cast_w2(on_scalar, 2, 44, P)
-        cast_w2(on_vector, 2, 0, 44)
-        quantize_y(0, 1)
+        cast_w2(on_vector, 2, 0, P)
+        quantize_y(0, 0, HALF)
         quantize_w2(2)
+        quantize_y(0, HALF, T)
         close_with_w2(2, (3, 0, 1, 2))
-        park(2, 3)
         store_codes(0, 1)
+        park(2, 3)
         gate_parked(2, 3)
-        gate(1, every, 0, HALF)
-        cast_y(on_scalar, 1, 0)
-        gate(1, every, HALF, T)
-        store_y(nc.scalar, 1)
-        cast_y(on_scalar, 1, 1)
-        gate(2, range(3), 0, HALF)
-        cast_y(on_scalar, 2, 0)
-        gate(2, range(3), HALF, T)
+        gate(1, every)
+        store_y(nc.sync, 1)
+        cast_y(on_scalar, 1)
+        gate(2, range(3))
         store_y(nc.sync, 2)
-        quantize_y(1, 0)
-        cast_y(on_vector, 2, 1)
-        quantize_y(1, 1)
-        quantize_y(2, 1)
-        quantize_y(2, 0)
+        cast_y(on_vector, 2, 0, 320)
+        cast_y(on_scalar, 2, 320, T)
+        quantize_y(1)
+        quantize_y(2)
         store_codes(1, 3)
         for r in range(4):
             nc.sync.dma_start(

@@ -215,41 +215,43 @@ def tile_mix_dconv_fm_pl_mul_kernel(
         deal_scales(1, 3)
         quantize_w2(0, 0, CH // 2)
         quantize_w2(0, CH // 2, CH)
-        close_with_w2(0, (0, 1, 3, 2))
+        close_with_w2(0, every)
         deal_w0(1, 3)
         open_with_w1(1, every)
         add_w0(1, every)
-        park(0, 3)
-        gate_parked(0, 3)
-        gate(0, range(3))
+        park(0, 0)
+        gate_parked(0, 0)
+        gate(0, range(1, 4))
         store_y(nc.sync, 0)
         open_with_w1(2, every)
         cast_w2(on_scalar, 1, 72, P)
         cast_w2(on_vector, 1, 0, 72)
         cast_y(on_scalar, 0, 0, HALF)
-        cast_y(on_scalar, 0, HALF, T)
         quantize_w2(1)
-        add_w0(2, range(2))
-        close_with_w2(1, every)
-        add_w0(2, range(2, 4))
-        cast_w2(on_vector, 2, 0, P)
+        close_with_w2(1, (3, 0, 1, 2))
+        add_w0(2, every)
+        cast_w2(on_vector, 2, 0, 96)
+        cast_w2(on_scalar, 2, 96, P)
         quantize_y(0, 0, HALF)
         quantize_w2(2)
-        quantize_y(0, HALF, T)
         close_with_w2(2, (3, 0, 1, 2))
-        store_codes(0, 1)
+        park(1, 3)
+        cast_y(on_scalar, 0, HALF, T)
         park(2, 3)
-        gate_parked(2, 3)
-        gate(1, every)
+        gate_parked(1, 3, 0, HALF)
+        gate_parked(1, 3, HALF, T)
+        gate(1, range(3))
         store_y(nc.sync, 1)
         cast_y(on_scalar, 1)
+        quantize_y(0, HALF, T)
+        gate_parked(2, 3)
         gate(2, range(3))
         store_y(nc.sync, 2)
-        cast_y(on_vector, 2, 0, 320)
-        cast_y(on_scalar, 2, 320, T)
+        cast_y(on_vector, 2, 0, 336)
+        cast_y(on_scalar, 2, 336, T)
         quantize_y(1)
         quantize_y(2)
-        store_codes(1, 3)
+        store_codes(0, 3)
         for r in range(4):
             nc.sync.dma_start(
                 out=out_2[:, r:16:4, :].rearrange("a q t -> q a t").bitcast(I32),

@@ -241,7 +241,7 @@ def tile_mix_dconv_fm_pl_mul_kernel(
         gate_parked(1, 3, 0, HALF)
         gate_parked(1, 3, HALF, T)
         gate(1, range(3))
-        store_y(nc.sync, 1)
+        store_y(nc.scalar, 1)
         cast_y(on_scalar, 1)
         quantize_y(0, HALF, T)
         gate_parked(2, 3)
@@ -251,9 +251,9 @@ def tile_mix_dconv_fm_pl_mul_kernel(
         cast_y(on_scalar, 2, 336, T)
         quantize_y(1)
         quantize_y(2)
-        store_codes(0, 3)
         for r in range(4):
             nc.sync.dma_start(
                 out=out_2[:, r:16:4, :].rearrange("a q t -> q a t").bitcast(I32),
                 in_=o_scales[OUT_ROW + r : P : 32, :, :].bitcast(I32),
             )
+        store_codes(0, 3)

@@ -58,7 +58,8 @@ def tile_mix_dconv_fm_pl_mul_kernel(
         w2_codes = [tile("w2_codes%d" % a, [P, CH], U32) for a in range(NCH)]
         w2_scales = [tile("w2_scales%d" % a, [P, CH], U8) for a in range(NCH)]
         g_sb = [tile("g_sb%d" % a, [P, PACK, T], F32) for a in range(NCH)]
-        y_sb = [tile("y_sb%d" % a, [P, PACK, T], F32) for a in range(NCH)]
+        y_all = tile("y_all", [P, NCH, PACK, T], F32)
+        y_sb = [y_all[:, a, :, :] for a in range(NCH)]
         y_bf = [tile("y_bf%d" % a, [P, T, PACK], BF16) for a in range(NCH)]
         o_codes, o_scales = tile("o_codes", [P, NCH, T], U32), tile("o_scales", [P, NCH, T], U8)
 
@@ -121,23 +122,24 @@ def tile_mix_dconv_fm_pl_mul_kernel(
 
         banks = {}
 
-        def tap(a, r, codes, scales, t0, start=False, stop=False):
+        def tap(a, r, codes, scales, shift, start=False, stop=False, t0=0, t1=T):
             nc.tensor.matmul_mx(
-                out=banks[a, r][:],
+                out=banks[a, r][:, t0:t1],
                 lhsT=codes,
                 lhsT_scale=scales,
-                rhs=x_codes[:, t0 : t0 + T].bitcast(FP8X4),
-                rhs_scale=x_scales[:, t0 : t0 + T],
+                rhs=x_codes[:, shift + t0 : shift + t1].bitcast(FP8X4),
+                rhs_scale=x_scales[:, shift + t0 : shift + t1],
                 start=start,
                 stop=stop,
             )
 
-        def open_with_w1(a, rows):
+        def w1_pass(a, rows, start=True, t0=0, t1=T):
             for r in rows:
                 s = PACK * a + r
-                banks[a, r] = psum.tile([P, T], F32, name="bank%d" % (s % BANKS))
+                if start:
+                    banks[a, r] = psum.tile([P, T], F32, name="bank%d" % (s % BANKS))
                 cols = slice(s * P, (s + 1) * P)
-                tap(a, r, w1_codes[:, cols].bitcast(FP8X4), ws[W1_ROW:P, cols], D, start=True)
+                tap(a, r, w1_codes[:, cols].bitcast(FP8X4), ws[W1_ROW:P, cols], D, start=start, t0=t0, t1=t1)
 
         def add_w0(a, rows):
             for r in rows:
@@ -170,12 +172,12 @@ def tile_mix_dconv_fm_pl_mul_kernel(
         def quantize_y(a, t0=0, t1=T):
             quantize(y_bf[a][:, t0:t1, :], o_codes[:, a, t0:t1], o_scales[OUT_ROW:P, a, t0:t1])
 
-        def store_y(queue, a):
-            rows = out_0[a * CH : (a + 1) * CH, :]
-            queue.dma_start(out=rows.rearrange("(p r) t -> p r t", r=PACK), in_=y_sb[a][:])
+        def store_y(queue, a0, a1):
+            rows = out_0[a0 * CH : a1 * CH, :].rearrange("(a p r) t -> p a (r t)", p=P, r=PACK)
+            queue.dma_start(out=rows, in_=y_all[:, a0:a1, :, :].rearrange("p a r t -> p a (r t)"))
 
-        def store_codes(a0, a1):
-            nc.scalar.dma_start(
+        def store_codes(queue, a0, a1):
+            queue.dma_start(
                 out=out_1[a0:a1].rearrange("a p t i -> p a (t i)").bitcast(I32),
                 in_=o_codes[:, a0:a1, :].bitcast(I32),
             )
@@ -189,71 +191,72 @@ def tile_mix_dconv_fm_pl_mul_kernel(
         for r in range(2, 4):
             load_scale_rows(r)
         nc.sync.dma_start(out=w0_raw[:].bitcast(I32), in_=w0_words[0].bitcast(I32))
-        load_w2(0)
-        load_g(0)
-        load_w2(1)
-        load_w2(2)
-        load_g(1)
-        load_g(2)
+        for a in range(NCH):
+            load_w2(a)
+            load_g(a)
 
         for a in range(NCH):
             deal_w1(a)
         cast_x(on_vector, 1)
-        cast_x(on_scalar, 2)
-        cast_x(on_scalar, 3)
+        for q in (2, 0, 3):
+            cast_x(on_scalar, q)
         deal_scales(0, 1)
         quantize_x(1)
+        w1_pass(0, every, True, 0, HALF)
         quantize_x(2)
-        open_with_w1(0, every)
-        cast_x(on_vector, 0)
+        w1_pass(0, every, False, HALF, T)
         deal_w0(0, 1)
-        quantize_x(0)
-        add_w0(0, every)
-        quantize_x(3)
-        cast_w2(on_vector, 0, 0, 84)
-        cast_w2(on_scalar, 0, 84, P)
         deal_scales(1, 3)
-        quantize_w2(0, 0, CH // 2)
-        quantize_w2(0, CH // 2, CH)
-        close_with_w2(0, every)
+        quantize_x(0)
+        add_w0(0, range(2))
         deal_w0(1, 3)
-        open_with_w1(1, every)
+        cast_w2(on_vector, 0, 0, 104)
+        cast_w2(on_scalar, 0, 104, P)
+        quantize_x(3)
+        quantize_w2(0, 0, CH // 2)
+        close_with_w2(0, range(2))
+        quantize_w2(0, CH // 2, CH)
+        for r in range(2, 4):
+            add_w0(0, [r])
+            close_with_w2(0, [r])
+        w1_pass(1, every)
         add_w0(1, every)
         park(0, 0)
         gate_parked(0, 0)
         gate(0, range(1, 4))
-        store_y(nc.sync, 0)
-        open_with_w1(2, every)
         cast_w2(on_scalar, 1, 72, P)
         cast_w2(on_vector, 1, 0, 72)
-        cast_y(on_scalar, 0, 0, HALF)
-        quantize_w2(1)
-        close_with_w2(1, (3, 0, 1, 2))
+        quantize_w2(1, 0, CH // 2)
+        quantize_w2(1, CH // 2, CH)
+        close_with_w2(1, every)
+        w1_pass(2, every)
         add_w0(2, every)
-        cast_w2(on_vector, 2, 0, 96)
-        cast_w2(on_scalar, 2, 96, P)
+        cast_y(on_scalar, 0, 0, P)
+        park(1, 0)
+        gate_parked(1, 0)
+        gate(1, range(1, 4))
+        store_y(nc.sync, 0, 2)
+        cast_y(on_scalar, 0, P, T)
+        cast_w2(on_scalar, 2, 84, P)
+        cast_w2(on_vector, 2, 0, 84)
         quantize_y(0, 0, HALF)
-        quantize_w2(2)
-        close_with_w2(2, (3, 0, 1, 2))
-        park(1, 3)
-        cast_y(on_scalar, 0, HALF, T)
-        park(2, 3)
-        gate_parked(1, 3, 0, HALF)
-        gate_parked(1, 3, HALF, T)
-        gate(1, range(3))
-        store_y(nc.scalar, 1)
-        cast_y(on_scalar, 1)
+        quantize_w2(2, 0, CH // 2)
+        quantize_w2(2, CH // 2, CH)
+        close_with_w2(2, every)
         quantize_y(0, HALF, T)
-        gate_parked(2, 3)
-        gate(2, range(3))
-        store_y(nc.sync, 2)
-        cast_y(on_vector, 2, 0, 336)
-        cast_y(on_scalar, 2, 336, T)
+        cast_y(on_scalar, 1, 0, P)
+        park(2, 0)
+        gate_parked(2, 0)
+        cast_y(on_scalar, 1, P, T)
+        gate(2, range(1, 4))
+        store_y(nc.scalar, 2, 3)
+        cast_y(on_scalar, 2, 320, T)
+        cast_y(on_vector, 2, 0, 320)
         quantize_y(1)
         quantize_y(2)
+        store_codes(nc.sync, 0, 3)
         for r in range(4):
             nc.sync.dma_start(
                 out=out_2[:, r:16:4, :].rearrange("a q t -> q a t").bitcast(I32),
                 in_=o_scales[OUT_ROW + r : P : 32, :, :].bitcast(I32),
             )
-        store_codes(0, 3)

@@ -22,6 +22,7 @@ CH = P * PACK
 NCH = M // CH
 HALF = T // 2
 BANKS = 8
+REUSED = (0, 1, 2, 7)
 W1_ROW = 4
 OUT_ROW = 8
 ALIGN = 256
@@ -137,7 +138,7 @@ def tile_mix_dconv_fm_pl_mul_kernel(
             for r in rows:
                 s = PACK * a + r
                 if start:
-                    banks[a, r] = psum.tile([P, T], F32, name="bank%d" % (s % BANKS))
+                    banks[a, r] = psum.tile([P, T], F32, name="bank%d" % (s if s < BANKS else REUSED[r]))
                 cols = slice(s * P, (s + 1) * P)
                 tap(a, r, w1_codes[:, cols].bitcast(FP8X4), ws[W1_ROW:P, cols], D, start=start, t0=t0, t1=t1)
 
@@ -158,8 +159,8 @@ def tile_mix_dconv_fm_pl_mul_kernel(
                     out=y_sb[a][:, r, t0:t1], in0=banks[a, r][:, t0:t1], in1=g_sb[a][:, r, t0:t1], op=MULT
                 )
 
-        def park(a, r):
-            nc.scalar.copy(out=y_sb[a][:, r, :], in_=banks[a, r][:])
+        def park(a, r, t0=0, t1=T):
+            nc.scalar.copy(out=y_sb[a][:, r, t0:t1], in_=banks[a, r][:, t0:t1])
 
         def gate_parked(a, r, t0=0, t1=T):
             nc.gpsimd.tensor_tensor(
@@ -191,9 +192,12 @@ def tile_mix_dconv_fm_pl_mul_kernel(
         for r in range(2, 4):
             load_scale_rows(r)
         nc.sync.dma_start(out=w0_raw[:].bitcast(I32), in_=w0_words[0].bitcast(I32))
-        for a in range(NCH):
-            load_w2(a)
-            load_g(a)
+        load_w2(0)
+        load_w2(1)
+        load_g(0)
+        load_g(1)
+        load_w2(2)
+        load_g(2)
 
         for a in range(NCH):
             deal_w1(a)
@@ -208,53 +212,57 @@ def tile_mix_dconv_fm_pl_mul_kernel(
         deal_w0(0, 1)
         deal_scales(1, 3)
         quantize_x(0)
-        add_w0(0, range(2))
+        add_w0(0, every)
+        w1_pass(1, [0])
         deal_w0(1, 3)
         cast_w2(on_vector, 0, 0, 104)
         cast_w2(on_scalar, 0, 104, P)
         quantize_x(3)
         quantize_w2(0, 0, CH // 2)
-        close_with_w2(0, range(2))
         quantize_w2(0, CH // 2, CH)
-        for r in range(2, 4):
-            add_w0(0, [r])
-            close_with_w2(0, [r])
-        w1_pass(1, every)
-        add_w0(1, every)
+        close_with_w2(0, every)
+        cast_w2(on_vector, 1, 0, 84)
+        cast_w2(on_scalar, 1, 84, P)
+        quantize_w2(1)
+        w1_pass(1, range(1, 4))
+        for r in every:
+            add_w0(1, [r])
+            close_with_w2(1, [r])
         park(0, 0)
-        gate_parked(0, 0)
-        gate(0, range(1, 4))
-        cast_w2(on_scalar, 1, 72, P)
-        cast_w2(on_vector, 1, 0, 72)
-        quantize_w2(1, 0, CH // 2)
-        quantize_w2(1, CH // 2, CH)
-        close_with_w2(1, every)
-        w1_pass(2, every)
-        add_w0(2, every)
-        cast_y(on_scalar, 0, 0, P)
+        park(0, 1, HALF, T)
         park(1, 0)
+        gate_parked(0, 0, 0, HALF)
+        gate(0, range(1, 4), 0, HALF)
+        cast_y(on_scalar, 0, 0, HALF)
+        for r in range(2):
+            gate_parked(0, r, HALF, T)
+        gate(0, range(2, 4), HALF, T)
+        cast_y(on_scalar, 0, HALF, T)
         gate_parked(1, 0)
         gate(1, range(1, 4))
         store_y(nc.sync, 0, 2)
-        cast_y(on_scalar, 0, P, T)
+        for r in every:
+            w1_pass(2, [r])
+            add_w0(2, [r])
+        quantize_y(0, 0, HALF)
         cast_w2(on_scalar, 2, 84, P)
         cast_w2(on_vector, 2, 0, 84)
-        quantize_y(0, 0, HALF)
         quantize_w2(2, 0, CH // 2)
         quantize_w2(2, CH // 2, CH)
         close_with_w2(2, every)
         quantize_y(0, HALF, T)
         cast_y(on_scalar, 1, 0, P)
-        park(2, 0)
-        gate_parked(2, 0)
+        for t0 in (0, HALF):
+            park(2, 0, t0, t0 + HALF)
+            gate_parked(2, 0, t0, t0 + HALF)
         cast_y(on_scalar, 1, P, T)
         gate(2, range(1, 4))
-        store_y(nc.scalar, 2, 3)
+        store_y(nc.sync, 2, 3)
         cast_y(on_scalar, 2, 320, T)
         cast_y(on_vector, 2, 0, 320)
         quantize_y(1)
         quantize_y(2)
-        store_codes(nc.sync, 0, 3)
+        store_codes(nc.scalar, 0, 3)
         for r in range(4):
             nc.sync.dma_start(
                 out=out_2[:, r:16:4, :].rearrange("a q t -> q a t").bitcast(I32),

@@ -213,31 +213,30 @@ def tile_mix_dconv_fm_pl_mul_kernel(
         deal_scales(1, 3)
         quantize_x(0)
         add_w0(0, every)
-        w1_pass(1, [0])
+        w1_pass(1, every)
         deal_w0(1, 3)
-        cast_w2(on_vector, 0, 0, 104)
-        cast_w2(on_scalar, 0, 104, P)
+        cast_w2(on_vector, 0, 0, 88)
+        cast_w2(on_scalar, 0, 88, P)
         quantize_x(3)
-        quantize_w2(0, 0, CH // 2)
-        quantize_w2(0, CH // 2, CH)
-        close_with_w2(0, every)
+        quantize_w2(0)
+        close_with_w2(0, range(1, 4))
         cast_w2(on_vector, 1, 0, 84)
         cast_w2(on_scalar, 1, 84, P)
-        quantize_w2(1)
-        w1_pass(1, range(1, 4))
+        quantize_w2(1, 0, CH // 2)
+        quantize_w2(1, CH // 2, CH)
         for r in every:
             add_w0(1, [r])
             close_with_w2(1, [r])
-        park(0, 0)
-        park(0, 1, HALF, T)
+            if r == 0:
+                close_with_w2(0, [0])
+        for t0 in (0, HALF):
+            park(0, 0, t0, t0 + HALF)
+            gate_parked(0, 0, t0, t0 + HALF)
         park(1, 0)
-        gate_parked(0, 0, 0, HALF)
-        gate(0, range(1, 4), 0, HALF)
-        cast_y(on_scalar, 0, 0, HALF)
-        for r in range(2):
-            gate_parked(0, r, HALF, T)
-        gate(0, range(2, 4), HALF, T)
-        cast_y(on_scalar, 0, HALF, T)
+        gate(0, range(1, 3))
+        for t0 in (0, HALF):
+            gate(0, [3], t0, t0 + HALF)
+            cast_y(on_scalar, 0, t0, t0 + HALF)
         gate_parked(1, 0)
         gate(1, range(1, 4))
         store_y(nc.sync, 0, 2)

@@ -22,7 +22,7 @@ CH = P * PACK
 NCH = M // CH
 HALF = T // 2
 BANKS = 8
-REUSED = (0, 1, 2, 7)
+REUSED = (0, 1, 6, 7)
 W1_ROW = 4
 OUT_ROW = 8
 ALIGN = 256
@@ -213,8 +213,8 @@ def tile_mix_dconv_fm_pl_mul_kernel(
         deal_scales(1, 3)
         quantize_x(0)
         add_w0(0, every)
-        w1_pass(1, every)
-        deal_w0(1, 3)
+        w1_pass(1, range(2))
+        deal_w0(1, 2)
         cast_w2(on_vector, 0, 0, 88)
         cast_w2(on_scalar, 0, 88, P)
         quantize_x(3)
@@ -224,18 +224,25 @@ def tile_mix_dconv_fm_pl_mul_kernel(
         cast_w2(on_scalar, 1, 84, P)
         quantize_w2(1, 0, CH // 2)
         quantize_w2(1, CH // 2, CH)
-        for r in every:
+        deal_w0(2, 3)
+        add_w0(1, [0])
+        close_with_w2(1, [0])
+        close_with_w2(0, [0])
+        add_w0(1, [1])
+        close_with_w2(1, [1])
+        for r in range(2, 4):
+            w1_pass(1, [r])
             add_w0(1, [r])
             close_with_w2(1, [r])
-            if r == 0:
-                close_with_w2(0, [0])
+        park(0, 1, HALF, T)
         for t0 in (0, HALF):
             park(0, 0, t0, t0 + HALF)
             gate_parked(0, 0, t0, t0 + HALF)
+        gate_parked(0, 1, HALF, T)
         park(1, 0)
-        gate(0, range(1, 3))
+        gate(0, [1], 0, HALF)
+        gate(0, range(2, 4))
         for t0 in (0, HALF):
-            gate(0, [3], t0, t0 + HALF)
             cast_y(on_scalar, 0, t0, t0 + HALF)
         gate_parked(1, 0)
         gate(1, range(1, 4))

@@ -234,15 +234,13 @@ def tile_mix_dconv_fm_pl_mul_kernel(
             w1_pass(1, [r])
             add_w0(1, [r])
             close_with_w2(1, [r])
-        park(0, 1, HALF, T)
         for t0 in (0, HALF):
             park(0, 0, t0, t0 + HALF)
             gate_parked(0, 0, t0, t0 + HALF)
-        gate_parked(0, 1, HALF, T)
         park(1, 0)
-        gate(0, [1], 0, HALF)
-        gate(0, range(2, 4))
+        gate(0, range(1, 3))
         for t0 in (0, HALF):
+            gate(0, [3], t0, t0 + HALF)
             cast_y(on_scalar, 0, t0, t0 + HALF)
         gate_parked(1, 0)
         gate(1, range(1, 4))
@@ -258,17 +256,17 @@ def tile_mix_dconv_fm_pl_mul_kernel(
         close_with_w2(2, every)
         quantize_y(0, HALF, T)
         cast_y(on_scalar, 1, 0, P)
-        for t0 in (0, HALF):
-            park(2, 0, t0, t0 + HALF)
-            gate_parked(2, 0, t0, t0 + HALF)
+        park(2, 0, 0, 416)
+        gate_parked(2, 0, 0, 416)
         cast_y(on_scalar, 1, P, T)
         gate(2, range(1, 4))
+        gate(2, [0], 416, T)
         store_y(nc.sync, 2, 3)
         cast_y(on_scalar, 2, 320, T)
         cast_y(on_vector, 2, 0, 320)
         quantize_y(1)
         quantize_y(2)
-        store_codes(nc.scalar, 0, 3)
+        store_codes(nc.sync, 0, 3)
         for r in range(4):
             nc.sync.dma_start(
                 out=out_2[:, r:16:4, :].rearrange("a q t -> q a t").bitcast(I32),

@@ -22,7 +22,6 @@ CH = P * PACK
 NCH = M // CH
 HALF = T // 2
 BANKS = 8
-REUSED = (0, 1, 6, 7)
 W1_ROW = 4
 OUT_ROW = 8
 ALIGN = 256
@@ -52,9 +51,10 @@ def tile_mix_dconv_fm_pl_mul_kernel(
         w1_raw, w1_codes = tile("w1_raw", [P, M], I32), tile("w1_codes", [P, M], U32)
         ws_raw, ws = tile("ws_raw", [P, M], U8), tile("ws", [P, M], U8)
         x_raw = tile("x_raw", [P, PACK, XW], F32)
-        x_bf = [tile("x_bf%d" % q, [P, D, PACK], BF16) for q in range(XW // D)]
+        x_bf = [tile("x_bf%d" % h, [P, T, PACK], BF16) for h in range(XW // T)]
         x_codes, x_scales = tile("x_codes", [P, XW], U32), tile("x_scales", [P, XW], U8)
-        w2_raw = [tile("w2_raw%d" % a, [P, PACK, CH], F32) for a in range(NCH)]
+        w2_first, w2_last = tile("w2_first", [P, PACK, 2 * CH], F32), tile("w2_last", [P, PACK, CH], F32)
+        w2_raw = [w2_first[:, :, :CH], w2_first[:, :, CH:], w2_last[:]]
         w2_bf = [tile("w2_bf%d" % a, [P, CH, PACK], BF16) for a in range(NCH)]
         w2_codes = [tile("w2_codes%d" % a, [P, CH], U32) for a in range(NCH)]
         w2_scales = [tile("w2_scales%d" % a, [P, CH], U8) for a in range(NCH)]
@@ -70,9 +70,9 @@ def tile_mix_dconv_fm_pl_mul_kernel(
                     out=ws_raw[row0 + r : P : 32, :].bitcast(I32), in_=src[0, r:16:4, :].bitcast(I32)
                 )
 
-        def load_w2(a):
+        def load_w2(dst, a0, a1):
             rows = w2.rearrange("(p j) n -> p j n", j=PACK)
-            nc.sync.dma_start(out=w2_raw[a][:], in_=rows[:, :, a * CH : (a + 1) * CH])
+            nc.sync.dma_start(out=dst[:], in_=rows[:, :, a0 * CH : a1 * CH])
 
         def load_g(a):
             rows = g[a * CH : (a + 1) * CH, :]
@@ -81,22 +81,22 @@ def tile_mix_dconv_fm_pl_mul_kernel(
         def deal_w0(a0, a1):
             cols = slice(2 * a0 * CH, 2 * a1 * CH)
             nc.vector.tensor_copy(
-                out=w0_codes[:, cols].bitcast(U16).rearrange("p (a r c i) -> p a c r i", r=PACK, c=16, i=8),
-                in_=w0_raw[:, cols].bitcast(U16).rearrange("p (a c i r) -> p a c r i", r=PACK, c=16, i=8),
+                out=w0_codes[:, cols].bitcast(U16).rearrange("p (a r c i) -> p c a r i", r=PACK, c=16, i=8),
+                in_=w0_raw[:, cols].bitcast(U16).rearrange("p (a c i r) -> p c a r i", r=PACK, c=16, i=8),
             )
 
-        def deal_w1(a):
-            cols = slice(a * CH, (a + 1) * CH)
-            nc.vector.tensor_copy(
-                out=w1_codes[:, cols].bitcast(I32).rearrange("p (r m) -> p m r", r=PACK),
-                in_=w1_raw[:, cols].rearrange("p (m r) -> p m r", r=PACK),
+        def deal_w1(copy, a0, a1):
+            cols = slice(a0 * CH, a1 * CH)
+            copy(
+                out=w1_codes[:, cols].rearrange("p (a r m) -> p a m r", r=PACK, m=P),
+                in_=w1_raw[:, cols].bitcast(U32).rearrange("p (a m r) -> p a m r", r=PACK, m=P),
             )
 
         def deal_scales(a0, a1):
             cols = slice(a0 * CH, a1 * CH)
             nc.vector.tensor_copy(
-                out=ws[:, cols].rearrange("p (a r m) -> p a r m", r=PACK, m=P),
-                in_=ws_raw[:, cols].rearrange("p (a m r) -> p a r m", r=PACK, m=P),
+                out=ws[:, cols].rearrange("p (a r m) -> p r a m", r=PACK, m=P),
+                in_=ws_raw[:, cols].rearrange("p (a m r) -> p r a m", r=PACK, m=P),
             )
 
         def quantize(grouped, codes, scales):
@@ -104,17 +104,18 @@ def tile_mix_dconv_fm_pl_mul_kernel(
                 out=codes.bitcast(FP8X4), scales=scales, in_=grouped.rearrange("p c j -> p (c j)")
             )
 
-        def cast_x(copy, q):
-            interleave(copy, x_bf[q][:], x_raw[:, :, q * D : (q + 1) * D])
+        def cast_x(copy, c0, c1):
+            h = c0 // T
+            interleave(copy, x_bf[h][:, c0 - h * T : c1 - h * T, :], x_raw[:, :, c0:c1])
 
-        def quantize_x(q):
-            cols = slice(q * D, (q + 1) * D)
-            quantize(x_bf[q][:], x_codes[:, cols], x_scales[:, cols])
+        def quantize_x(h):
+            cols = slice(h * T, (h + 1) * T)
+            quantize(x_bf[h][:], x_codes[:, cols], x_scales[:, cols])
 
         def cast_w2(copy, a, m0, m1):
             copy(
                 out=w2_bf[a][:].rearrange("p (r m) j -> p m j r", r=PACK)[:, m0:m1, :, :],
-                in_=w2_raw[a][:].rearrange("p j (m r) -> p m j r", r=PACK)[:, m0:m1, :, :],
+                in_=w2_raw[a].rearrange("p j (m r) -> p m j r", r=PACK)[:, m0:m1, :, :],
             )
 
         def quantize_w2(a, c0=0, c1=CH):
@@ -123,35 +124,34 @@ def tile_mix_dconv_fm_pl_mul_kernel(
 
         banks = {}
 
-        def tap(a, r, codes, scales, shift, start=False, stop=False, t0=0, t1=T):
+        def tap(a, r, codes, scales, shift, start=False, stop=False):
             nc.tensor.matmul_mx(
-                out=banks[a, r][:, t0:t1],
+                out=banks[a, r][:],
                 lhsT=codes,
                 lhsT_scale=scales,
-                rhs=x_codes[:, shift + t0 : shift + t1].bitcast(FP8X4),
-                rhs_scale=x_scales[:, shift + t0 : shift + t1],
+                rhs=x_codes[:, shift : shift + T].bitcast(FP8X4),
+                rhs_scale=x_scales[:, shift : shift + T],
                 start=start,
                 stop=stop,
             )
 
-        def w1_pass(a, rows, start=True, t0=0, t1=T):
+        def open_with_w0(a, rows):
             for r in rows:
                 s = PACK * a + r
-                if start:
-                    banks[a, r] = psum.tile([P, T], F32, name="bank%d" % (s if s < BANKS else REUSED[r]))
-                cols = slice(s * P, (s + 1) * P)
-                tap(a, r, w1_codes[:, cols].bitcast(FP8X4), ws[W1_ROW:P, cols], D, start=start, t0=t0, t1=t1)
-
-        def add_w0(a, rows):
-            for r in rows:
-                s = PACK * a + r
+                banks[a, r] = psum.tile([P, T], F32, name="bank%d" % (s % BANKS))
                 codes = w0_codes[:, 2 * s * P : 2 * (s + 1) * P]
-                tap(a, r, codes.bitcast(FP4X4), ws[:, s * P : (s + 1) * P], 0)
+                tap(a, r, codes.bitcast(FP4X4), ws[:, s * P : (s + 1) * P], 0, start=True)
 
-        def close_with_w2(a, rows):
+        def w1_pass(a, rows, stop):
+            for r in rows:
+                s = PACK * a + r
+                cols = slice(s * P, (s + 1) * P)
+                tap(a, r, w1_codes[:, cols].bitcast(FP8X4), ws[W1_ROW:P, cols], D, stop=stop)
+
+        def w2_pass(a, rows, stop):
             for r in rows:
                 cols = slice(r * P, (r + 1) * P)
-                tap(a, r, w2_codes[a][:, cols].bitcast(FP8X4), w2_scales[a][:, cols], 2 * D, stop=True)
+                tap(a, r, w2_codes[a][:, cols].bitcast(FP8X4), w2_scales[a][:, cols], 2 * D, stop=stop)
 
         def gate(a, rows, t0=0, t1=T):
             for r in rows:
@@ -185,57 +185,40 @@ def tile_mix_dconv_fm_pl_mul_kernel(
 
         every = range(PACK)
         nc.vector.memset(ws_raw[:].bitcast(I32), 0)
-        nc.sync.dma_start(out=w1_raw[:], in_=w1_words[0].rearrange("p n i -> p (n i)").bitcast(I32))
-        for r in range(2):
-            load_scale_rows(r)
-        nc.sync.dma_start(out=x_raw[:], in_=x.rearrange("(p j) t -> p j t", j=PACK))
-        for r in range(2, 4):
-            load_scale_rows(r)
         nc.sync.dma_start(out=w0_raw[:].bitcast(I32), in_=w0_words[0].bitcast(I32))
-        load_w2(0)
-        load_w2(1)
+        load_scale_rows(0)
+        nc.sync.dma_start(out=x_raw[:], in_=x.rearrange("(p j) t -> p j t", j=PACK))
+        for r in range(1, 4):
+            load_scale_rows(r)
+        load_w2(w2_first, 0, 2)
+        nc.sync.dma_start(out=w1_raw[:], in_=w1_words[0].rearrange("p n i -> p (n i)").bitcast(I32))
         load_g(0)
         load_g(1)
-        load_w2(2)
+        load_w2(w2_last, 2, 3)
         load_g(2)
 
-        for a in range(NCH):
-            deal_w1(a)
-        cast_x(on_vector, 1)
-        for q in (2, 0, 3):
-            cast_x(on_scalar, q)
-        deal_scales(0, 1)
-        quantize_x(1)
-        w1_pass(0, every, True, 0, HALF)
-        quantize_x(2)
-        w1_pass(0, every, False, HALF, T)
-        deal_w0(0, 1)
-        deal_scales(1, 3)
+        deal_w0(0, 3)
+        cast_x(on_vector, 0, D)
+        cast_x(on_scalar, D, T)
+        deal_scales(0, 3)
+        cast_x(on_scalar, T, XW)
         quantize_x(0)
-        add_w0(0, every)
-        w1_pass(1, range(2))
-        deal_w0(1, 2)
-        cast_w2(on_vector, 0, 0, 88)
-        cast_w2(on_scalar, 0, 88, P)
-        quantize_x(3)
-        quantize_w2(0)
-        close_with_w2(0, range(1, 4))
-        cast_w2(on_vector, 1, 0, 84)
-        cast_w2(on_scalar, 1, 84, P)
-        quantize_w2(1, 0, CH // 2)
-        quantize_w2(1, CH // 2, CH)
-        deal_w0(2, 3)
-        add_w0(1, [0])
-        close_with_w2(1, [0])
-        close_with_w2(0, [0])
-        add_w0(1, [1])
-        close_with_w2(1, [1])
-        for r in range(2, 4):
-            w1_pass(1, [r])
-            add_w0(1, [r])
-            close_with_w2(1, [r])
+        open_with_w0(0, every)
+        open_with_w0(1, every)
+        quantize_x(1)
+        for a in range(2):
+            cast_w2(on_vector, a, 0, 84)
+            cast_w2(on_scalar, a, 84, P)
+            quantize_w2(a)
+        deal_w1(on_scalar, 0, 1)
+        deal_w1(on_vector, 1, 3)
+        w2_pass(0, every, False)
+        w1_pass(0, every, True)
+        for r in every:
+            w2_pass(1, [r], False)
+            w1_pass(1, [r], True)
+        park(0, 0)
         for t0 in (0, HALF):
-            park(0, 0, t0, t0 + HALF)
             gate_parked(0, 0, t0, t0 + HALF)
         park(1, 0)
         gate(0, range(1, 3))
@@ -246,14 +229,14 @@ def tile_mix_dconv_fm_pl_mul_kernel(
         gate(1, range(1, 4))
         store_y(nc.sync, 0, 2)
         for r in every:
-            w1_pass(2, [r])
-            add_w0(2, [r])
+            open_with_w0(2, [r])
+            w1_pass(2, [r], False)
         quantize_y(0, 0, HALF)
         cast_w2(on_scalar, 2, 84, P)
         cast_w2(on_vector, 2, 0, 84)
         quantize_w2(2, 0, CH // 2)
         quantize_w2(2, CH // 2, CH)
-        close_with_w2(2, every)
+        w2_pass(2, every, True)
         quantize_y(0, HALF, T)
         cast_y(on_scalar, 1, 0, P)
         park(2, 0, 0, 416)

@@ -49,7 +49,8 @@ def tile_mix_dconv_fm_pl_mul_kernel(
 
         w0_raw, w0_codes = tile("w0_raw", [P, 2 * M], U8), tile("w0_codes", [P, 2 * M], U8)
         w1_raw, w1_codes = tile("w1_raw", [P, M], I32), tile("w1_codes", [P, M], U32)
-        ws_raw, ws = tile("ws_raw", [P, M], U8), tile("ws", [P, M], U8)
+        ws_raw = tile("ws_raw", [P, 2, M], U8)
+        ws = [tile("ws%d" % w, [P, M], U8) for w in range(2)]
         x_raw = tile("x_raw", [P, PACK, XW], F32)
         x_bf = [tile("x_bf%d" % h, [P, T, PACK], BF16) for h in range(XW // T)]
         x_codes, x_scales = tile("x_codes", [P, XW], U32), tile("x_scales", [P, XW], U8)
@@ -64,10 +65,10 @@ def tile_mix_dconv_fm_pl_mul_kernel(
         y_bf = [tile("y_bf%d" % a, [P, T, PACK], BF16) for a in range(NCH)]
         o_codes, o_scales = tile("o_codes", [P, NCH, T], U32), tile("o_scales", [P, NCH, T], U8)
 
-        def load_scale_rows(r):
-            for src, row0 in ((w0_scales, 0), (w1_scales, W1_ROW)):
+        def load_scale_rows(w, src, row0):
+            for r in range(4):
                 nc.sync.dma_start(
-                    out=ws_raw[row0 + r : P : 32, :].bitcast(I32), in_=src[0, r:16:4, :].bitcast(I32)
+                    out=ws_raw[row0 + r : P : 32, w, :].bitcast(I32), in_=src[0, r:16:4, :].bitcast(I32)
                 )
 
         def load_w2(dst, a0, a1):
@@ -92,11 +93,11 @@ def tile_mix_dconv_fm_pl_mul_kernel(
                 in_=w1_raw[:, cols].bitcast(U32).rearrange("p (a m r) -> p a m r", r=PACK, m=P),
             )
 
-        def deal_scales(a0, a1):
+        def deal_scales(w, a0, a1):
             cols = slice(a0 * CH, a1 * CH)
             nc.vector.tensor_copy(
-                out=ws[:, cols].rearrange("p (a r m) -> p r a m", r=PACK, m=P),
-                in_=ws_raw[:, cols].rearrange("p (a m r) -> p r a m", r=PACK, m=P),
+                out=ws[w][:, cols].rearrange("p (a r m) -> p r a m", r=PACK, m=P),
+                in_=ws_raw[:, w, cols].rearrange("p (a m r) -> p r a m", r=PACK, m=P),
             )
 
         def quantize(grouped, codes, scales):
@@ -140,13 +141,13 @@ def tile_mix_dconv_fm_pl_mul_kernel(
                 s = PACK * a + r
                 banks[a, r] = psum.tile([P, T], F32, name="bank%d" % (s % BANKS))
                 codes = w0_codes[:, 2 * s * P : 2 * (s + 1) * P]
-                tap(a, r, codes.bitcast(FP4X4), ws[:, s * P : (s + 1) * P], 0, start=True)
+                tap(a, r, codes.bitcast(FP4X4), ws[0][:, s * P : (s + 1) * P], 0, start=True)
 
         def w1_pass(a, rows, stop):
             for r in rows:
                 s = PACK * a + r
                 cols = slice(s * P, (s + 1) * P)
-                tap(a, r, w1_codes[:, cols].bitcast(FP8X4), ws[W1_ROW:P, cols], D, stop=stop)
+                tap(a, r, w1_codes[:, cols].bitcast(FP8X4), ws[1][W1_ROW:P, cols], D, stop=stop)
 
         def w2_pass(a, rows, stop):
             for r in rows:
@@ -184,34 +185,38 @@ def tile_mix_dconv_fm_pl_mul_kernel(
             )
 
         every = range(PACK)
-        nc.vector.memset(ws_raw[:].bitcast(I32), 0)
-        nc.sync.dma_start(out=w0_raw[:].bitcast(I32), in_=w0_words[0].bitcast(I32))
-        load_scale_rows(0)
+        nc.vector.memset(ws_raw[:].rearrange("p w n -> p (w n)").bitcast(I32), 0)
         nc.sync.dma_start(out=x_raw[:], in_=x.rearrange("(p j) t -> p j t", j=PACK))
-        for r in range(1, 4):
-            load_scale_rows(r)
+        nc.sync.dma_start(out=w0_raw[:].bitcast(I32), in_=w0_words[0].bitcast(I32))
+        load_scale_rows(0, w0_scales, 0)
         load_w2(w2_first, 0, 2)
+        load_scale_rows(1, w1_scales, W1_ROW)
         nc.sync.dma_start(out=w1_raw[:], in_=w1_words[0].rearrange("p n i -> p (n i)").bitcast(I32))
         load_g(0)
         load_g(1)
         load_w2(w2_last, 2, 3)
         load_g(2)
 
-        deal_w0(0, 3)
         cast_x(on_vector, 0, D)
         cast_x(on_scalar, D, T)
-        deal_scales(0, 3)
         cast_x(on_scalar, T, XW)
+        deal_w0(0, 3)
         quantize_x(0)
+        deal_scales(0, 0, 3)
         open_with_w0(0, every)
         open_with_w0(1, every)
         quantize_x(1)
-        for a in range(2):
-            cast_w2(on_vector, a, 0, 84)
-            cast_w2(on_scalar, a, 84, P)
-            quantize_w2(a)
-        deal_w1(on_scalar, 0, 1)
-        deal_w1(on_vector, 1, 3)
+        cast_w2(on_vector, 0, 0, 84)
+        cast_w2(on_scalar, 0, 84, P)
+        deal_scales(1, 0, 1)
+        quantize_w2(0)
+        cast_w2(on_vector, 1, 0, 84)
+        cast_w2(on_scalar, 1, 84, P)
+        deal_scales(1, 1, 2)
+        quantize_w2(1)
+        deal_scales(1, 2, 3)
+        for a in range(NCH):
+            deal_w1(on_scalar, a, a + 1)
         w2_pass(0, every, False)
         w1_pass(0, every, True)
         for r in every:

@@ -230,9 +230,10 @@ def tile_mix_dconv_fm_pl_mul_kernel(
         for t0 in (0, HALF):
             gate(0, [3], t0, t0 + HALF)
             cast_y(on_scalar, 0, t0, t0 + HALF)
+        store_y(nc.sync, 0, 1)
         gate_parked(1, 0)
         gate(1, range(1, 4))
-        store_y(nc.sync, 0, 2)
+        store_y(nc.sync, 1, 2)
         for r in every:
             open_with_w0(2, [r])
             w1_pass(2, [r], False)

@@ -22,6 +22,7 @@ CH = P * PACK
 NCH = M // CH
 HALF = T // 2
 BANKS = 8
+REUSED = (0, 1, 6, 7)
 W1_ROW = 4
 OUT_ROW = 8
 ALIGN = 256
@@ -139,7 +140,7 @@ def tile_mix_dconv_fm_pl_mul_kernel(
         def open_with_w0(a, rows):
             for r in rows:
                 s = PACK * a + r
-                banks[a, r] = psum.tile([P, T], F32, name="bank%d" % (s % BANKS))
+                banks[a, r] = psum.tile([P, T], F32, name="bank%d" % (s if s < BANKS else REUSED[r]))
                 codes = w0_codes[:, 2 * s * P : 2 * (s + 1) * P]
                 tap(a, r, codes.bitcast(FP4X4), ws[0][:, s * P : (s + 1) * P], 0, start=True)
 

@@ -68,7 +68,7 @@ def tile_mix_dconv_fm_pl_mul_kernel(
 
         def load_scale_rows(w, src, row0):
             for r in range(4):
-                nc.sync.dma_start(
+                nc.scalar.dma_start(
                     out=ws_raw[row0 + r : P : 32, w, :].bitcast(I32), in_=src[0, r:16:4, :].bitcast(I32)
                 )
 
@@ -187,9 +187,9 @@ def tile_mix_dconv_fm_pl_mul_kernel(
 
         every = range(PACK)
         nc.vector.memset(ws_raw[:].rearrange("p w n -> p (w n)").bitcast(I32), 0)
+        load_scale_rows(0, w0_scales, 0)
         nc.sync.dma_start(out=x_raw[:], in_=x.rearrange("(p j) t -> p j t", j=PACK))
         nc.sync.dma_start(out=w0_raw[:].bitcast(I32), in_=w0_words[0].bitcast(I32))
-        load_scale_rows(0, w0_scales, 0)
         load_w2(w2_first, 0, 2)
         load_scale_rows(1, w1_scales, W1_ROW)
         nc.sync.dma_start(out=w1_raw[:], in_=w1_words[0].rearrange("p n i -> p (n i)").bitcast(I32))
@@ -198,24 +198,22 @@ def tile_mix_dconv_fm_pl_mul_kernel(
         load_w2(w2_last, 2, 3)
         load_g(2)
 
+        deal_scales(0, 0, 3)
         cast_x(on_vector, 0, D)
         cast_x(on_scalar, D, T)
         cast_x(on_scalar, T, XW)
         deal_w0(0, 3)
         quantize_x(0)
-        deal_scales(0, 0, 3)
         open_with_w0(0, every)
         open_with_w0(1, every)
         quantize_x(1)
+        deal_scales(1, 0, 3)
         cast_w2(on_vector, 0, 0, 84)
         cast_w2(on_scalar, 0, 84, P)
-        deal_scales(1, 0, 1)
         quantize_w2(0)
         cast_w2(on_vector, 1, 0, 84)
         cast_w2(on_scalar, 1, 84, P)
-        deal_scales(1, 1, 2)
         quantize_w2(1)
-        deal_scales(1, 2, 3)
         for a in range(NCH):
             deal_w1(on_scalar, a, a + 1)
         w2_pass(0, every, False)

@@ -66,9 +66,9 @@ def tile_mix_dconv_fm_pl_mul_kernel(
         y_bf = [tile("y_bf%d" % a, [P, T, PACK], BF16) for a in range(NCH)]
         o_codes, o_scales = tile("o_codes", [P, NCH, T], U32), tile("o_scales", [P, NCH, T], U8)
 
-        def load_scale_rows(w, src, row0):
+        def load_scale_rows(queue, w, src, row0):
             for r in range(4):
-                nc.scalar.dma_start(
+                queue.dma_start(
                     out=ws_raw[row0 + r : P : 32, w, :].bitcast(I32), in_=src[0, r:16:4, :].bitcast(I32)
                 )
 
@@ -187,11 +187,11 @@ def tile_mix_dconv_fm_pl_mul_kernel(
 
         every = range(PACK)
         nc.vector.memset(ws_raw[:].rearrange("p w n -> p (w n)").bitcast(I32), 0)
-        load_scale_rows(0, w0_scales, 0)
-        nc.sync.dma_start(out=x_raw[:], in_=x.rearrange("(p j) t -> p j t", j=PACK))
+        load_scale_rows(nc.scalar, 0, w0_scales, 0)
+        nc.sync.dma_start(out=x_raw[:], in_=x.rearrange("(p j) t -> p j t", j=PACK), max_dma_last_dim=2048)
         nc.sync.dma_start(out=w0_raw[:].bitcast(I32), in_=w0_words[0].bitcast(I32))
         load_w2(w2_first, 0, 2)
-        load_scale_rows(1, w1_scales, W1_ROW)
+        load_scale_rows(nc.sync, 1, w1_scales, W1_ROW)
         nc.sync.dma_start(out=w1_raw[:], in_=w1_words[0].rearrange("p n i -> p (n i)").bitcast(I32))
         load_g(0)
         load_g(1)
@@ -207,13 +207,15 @@ def tile_mix_dconv_fm_pl_mul_kernel(
         open_with_w0(0, every)
         open_with_w0(1, every)
         quantize_x(1)
-        deal_scales(1, 0, 3)
         cast_w2(on_vector, 0, 0, 84)
         cast_w2(on_scalar, 0, 84, P)
+        deal_scales(1, 0, 1)
         quantize_w2(0)
         cast_w2(on_vector, 1, 0, 84)
         cast_w2(on_scalar, 1, 84, P)
+        deal_scales(1, 1, 2)
         quantize_w2(1)
+        deal_scales(1, 2, 3)
         for a in range(NCH):
             deal_w1(on_scalar, a, a + 1)
         w2_pass(0, every, False)

@@ -188,7 +188,7 @@ def tile_mix_dconv_fm_pl_mul_kernel(
         every = range(PACK)
         nc.vector.memset(ws_raw[:].rearrange("p w n -> p (w n)").bitcast(I32), 0)
         load_scale_rows(nc.scalar, 0, w0_scales, 0)
-        nc.sync.dma_start(out=x_raw[:], in_=x.rearrange("(p j) t -> p j t", j=PACK), max_dma_last_dim=2048)
+        nc.sync.dma_start(out=x_raw[:], in_=x.rearrange("(p j) t -> p j t", j=PACK))
         nc.sync.dma_start(out=w0_raw[:].bitcast(I32), in_=w0_words[0].bitcast(I32))
         load_w2(w2_first, 0, 2)
         load_scale_rows(nc.sync, 1, w1_scales, W1_ROW)

@@ -66,9 +66,9 @@ def tile_mix_dconv_fm_pl_mul_kernel(
         y_bf = [tile("y_bf%d" % a, [P, T, PACK], BF16) for a in range(NCH)]
         o_codes, o_scales = tile("o_codes", [P, NCH, T], U32), tile("o_scales", [P, NCH, T], U8)
 
-        def load_scale_rows(queue, w, src, row0):
-            for r in range(4):
-                queue.dma_start(
+        def load_scale_rows(w, src, row0, rows):
+            for r in rows:
+                nc.scalar.dma_start(
                     out=ws_raw[row0 + r : P : 32, w, :].bitcast(I32), in_=src[0, r:16:4, :].bitcast(I32)
                 )
 
@@ -187,20 +187,21 @@ def tile_mix_dconv_fm_pl_mul_kernel(
 
         every = range(PACK)
         nc.vector.memset(ws_raw[:].rearrange("p w n -> p (w n)").bitcast(I32), 0)
-        load_scale_rows(nc.scalar, 0, w0_scales, 0)
+        load_scale_rows(0, w0_scales, 0, every)
         nc.sync.dma_start(out=x_raw[:], in_=x.rearrange("(p j) t -> p j t", j=PACK))
         nc.sync.dma_start(out=w0_raw[:].bitcast(I32), in_=w0_words[0].bitcast(I32))
         load_w2(w2_first, 0, 2)
-        load_scale_rows(nc.sync, 1, w1_scales, W1_ROW)
+        load_scale_rows(1, w1_scales, W1_ROW, [0])
+        deal_scales(0, 0, 3)
+        cast_x(on_vector, 0, D)
+        cast_x(on_scalar, D, T)
+        load_scale_rows(1, w1_scales, W1_ROW, [1, 2, 3])
         nc.sync.dma_start(out=w1_raw[:], in_=w1_words[0].rearrange("p n i -> p (n i)").bitcast(I32))
         load_g(0)
         load_g(1)
         load_w2(w2_last, 2, 3)
         load_g(2)
 
-        deal_scales(0, 0, 3)
-        cast_x(on_vector, 0, D)
-        cast_x(on_scalar, D, T)
         cast_x(on_scalar, T, XW)
         deal_w0(0, 3)
         quantize_x(0)

from contextlib import ExitStack

import concourse.mybir as mybir

D, K, M, T = 256, 512, 1536, 512
XW = T + 2 * D
FLOPS = 2 * 3 * K * M * T

F32 = mybir.dt.float32
BF16 = mybir.dt.bfloat16
I32 = mybir.dt.int32
U32 = mybir.dt.uint32
U16 = mybir.dt.uint16
U8 = mybir.dt.uint8
FP8X4 = mybir.dt.float8_e4m3fn_x4
FP4X4 = mybir.dt.float4_e2m1fn_x4
MULT = mybir.AluOpType.mult

P = 128
PACK = 4
CH = P * PACK
NCH = M // CH
HALF = T // 2
BANKS = 8
REUSED = (0, 1, 6, 7)
W1_ROW = 4
OUT_ROW = 8
ALIGN = 256


def interleave(copy, dst, src):
    copy(
        out=dst.rearrange("p (c i) j -> p c j i", i=4),
        in_=src.rearrange("p j (c i) -> p c j i", i=4),
    )


def tile_mix_dconv_fm_pl_mul_kernel(
    tc, x, w0_words, w0_scales, w1_words, w1_scales, w2, g, out_0, out_1, out_2
):
    nc = tc.nc
    with ExitStack() as ctx:
        sb = ctx.enter_context(tc.tile_pool(name="sb", bufs=1))
        psum = ctx.enter_context(tc.psum_pool(name="psum", bufs=1))
        ctx.enter_context(tc.manual_schedule())
        on_vector, on_scalar = nc.vector.tensor_copy, nc.scalar.copy

        def tile(name, shape, dtype):
            return sb.tile(shape, dtype, name=name, align_bytes=ALIGN)

        w0_raw, w0_codes = tile("w0_raw", [P, 2 * M], U8), tile("w0_codes", [P, 2 * M], U8)
        w1_raw, w1_codes = tile("w1_raw", [P, M], I32), tile("w1_codes", [P, M], U32)
        ws_raw = tile("ws_raw", [P, 2, M], U8)
        ws = [tile("ws%d" % w, [P, M], U8) for w in range(2)]
        x_raw = tile("x_raw", [P, PACK, XW], F32)
        x_bf = [tile("x_bf%d" % h, [P, T, PACK], BF16) for h in range(XW // T)]
        x_codes, x_scales = tile("x_codes", [P, XW], U32), tile("x_scales", [P, XW], U8)
        w2_first, w2_last = tile("w2_first", [P, PACK, 2 * CH], F32), tile("w2_last", [P, PACK, CH], F32)
        w2_raw = [w2_first[:, :, :CH], w2_first[:, :, CH:], w2_last[:]]
        w2_bf = [tile("w2_bf%d" % a, [P, CH, PACK], BF16) for a in range(NCH)]
        w2_codes = [tile("w2_codes%d" % a, [P, CH], U32) for a in range(NCH)]
        w2_scales = [tile("w2_scales%d" % a, [P, CH], U8) for a in range(NCH)]
        g_sb = [tile("g_sb%d" % a, [P, PACK, T], F32) for a in range(NCH)]
        y_all = tile("y_all", [P, NCH, PACK, T], F32)
        y_sb = [y_all[:, a, :, :] for a in range(NCH)]
        y_bf = [tile("y_bf%d" % a, [P, T, PACK], BF16) for a in range(NCH)]
        o_codes, o_scales = tile("o_codes", [P, NCH, T], U32), tile("o_scales", [P, NCH, T], U8)

        def load_scale_rows(w, src, row0, rows):
            for r in rows:
                nc.scalar.dma_start(
                    out=ws_raw[row0 + r : P : 32, w, :].bitcast(I32), in_=src[0, r:16:4, :].bitcast(I32)
                )

        def load_w2(dst, a0, a1):
            rows = w2.rearrange("(p j) n -> p j n", j=PACK)
            nc.sync.dma_start(out=dst[:], in_=rows[:, :, a0 * CH : a1 * CH])

        def load_g(a):
            rows = g[a * CH : (a + 1) * CH, :]
            nc.sync.dma_start(out=g_sb[a][:], in_=rows.rearrange("(p r) t -> p r t", r=PACK))

        def deal_w0(a0, a1):
            cols = slice(2 * a0 * CH, 2 * a1 * CH)
            nc.vector.tensor_copy(
                out=w0_codes[:, cols].bitcast(U16).rearrange("p (a r c i) -> p c a r i", r=PACK, c=16, i=8),
                in_=w0_raw[:, cols].bitcast(U16).rearrange("p (a c i r) -> p c a r i", r=PACK, c=16, i=8),
            )

        def deal_w1(copy, a0, a1):
            cols = slice(a0 * CH, a1 * CH)
            copy(
                out=w1_codes[:, cols].rearrange("p (a r m) -> p a m r", r=PACK, m=P),
                in_=w1_raw[:, cols].bitcast(U32).rearrange("p (a m r) -> p a m r", r=PACK, m=P),
            )

        def deal_scales(w, a0, a1):
            cols = slice(a0 * CH, a1 * CH)
            nc.vector.tensor_copy(
                out=ws[w][:, cols].rearrange("p (a r m) -> p r a m", r=PACK, m=P),
                in_=ws_raw[:, w, cols].rearrange("p (a m r) -> p r a m", r=PACK, m=P),
            )

        def quantize(grouped, codes, scales):
            nc.vector.quantize_mx(
                out=codes.bitcast(FP8X4), scales=scales, in_=grouped.rearrange("p c j -> p (c j)")
            )

        def cast_x(copy, c0, c1):
            h = c0 // T
            interleave(copy, x_bf[h][:, c0 - h * T : c1 - h * T, :], x_raw[:, :, c0:c1])

        def quantize_x(h):
            cols = slice(h * T, (h + 1) * T)
            quantize(x_bf[h][:], x_codes[:, cols], x_scales[:, cols])

        def cast_w2(copy, a, m0, m1):
            copy(
                out=w2_bf[a][:].rearrange("p (r m) j -> p m j r", r=PACK)[:, m0:m1, :, :],
                in_=w2_raw[a].rearrange("p j (m r) -> p m j r", r=PACK)[:, m0:m1, :, :],
            )

        def quantize_w2(a, c0=0, c1=CH):
            cols = slice(c0, c1)
            quantize(w2_bf[a][:, cols, :], w2_codes[a][:, cols], w2_scales[a][:, cols])

        banks = {}

        def tap(a, r, codes, scales, shift, start=False, stop=False):
            nc.tensor.matmul_mx(
                out=banks[a, r][:],
                lhsT=codes,
                lhsT_scale=scales,
                rhs=x_codes[:, shift : shift + T].bitcast(FP8X4),
                rhs_scale=x_scales[:, shift : shift + T],
                start=start,
                stop=stop,
            )

        def open_with_w0(a, rows):
            for r in rows:
                s = PACK * a + r
                banks[a, r] = psum.tile([P, T], F32, name="bank%d" % (s if s < BANKS else REUSED[r]))
                codes = w0_codes[:, 2 * s * P : 2 * (s + 1) * P]
                tap(a, r, codes.bitcast(FP4X4), ws[0][:, s * P : (s + 1) * P], 0, start=True)

        def w1_pass(a, rows, stop):
            for r in rows:
                s = PACK * a + r
                cols = slice(s * P, (s + 1) * P)
                tap(a, r, w1_codes[:, cols].bitcast(FP8X4), ws[1][W1_ROW:P, cols], D, stop=stop)

        def w2_pass(a, rows, stop):
            for r in rows:
                cols = slice(r * P, (r + 1) * P)
                tap(a, r, w2_codes[a][:, cols].bitcast(FP8X4), w2_scales[a][:, cols], 2 * D, stop=stop)

        def gate(a, rows, t0=0, t1=T):
            for r in rows:
                nc.vector.tensor_tensor(
                    out=y_sb[a][:, r, t0:t1], in0=banks[a, r][:, t0:t1], in1=g_sb[a][:, r, t0:t1], op=MULT
                )

        def park(a, r, t0=0, t1=T):
            nc.scalar.copy(out=y_sb[a][:, r, t0:t1], in_=banks[a, r][:, t0:t1])

        def gate_parked(a, r, t0=0, t1=T):
            nc.gpsimd.tensor_tensor(
                out=y_sb[a][:, r, t0:t1], in0=y_sb[a][:, r, t0:t1], in1=g_sb[a][:, r, t0:t1], op=MULT
            )

        def cast_y(copy, a, t0=0, t1=T):
            interleave(copy, y_bf[a][:, t0:t1, :], y_sb[a][:, :, t0:t1])

        def quantize_y(a, t0=0, t1=T):
            quantize(y_bf[a][:, t0:t1, :], o_codes[:, a, t0:t1], o_scales[OUT_ROW:P, a, t0:t1])

        def store_y(queue, a0, a1):
            rows = out_0[a0 * CH : a1 * CH, :].rearrange("(a p r) t -> p a (r t)", p=P, r=PACK)
            queue.dma_start(out=rows, in_=y_all[:, a0:a1, :, :].rearrange("p a r t -> p a (r t)"))

        def store_codes(queue, a0, a1):
            queue.dma_start(
                out=out_1[a0:a1].rearrange("a p t i -> p a (t i)").bitcast(I32),
                in_=o_codes[:, a0:a1, :].bitcast(I32),
            )

        every = range(PACK)
        nc.vector.memset(ws_raw[:].rearrange("p w n -> p (w n)").bitcast(I32), 0)
        load_scale_rows(0, w0_scales, 0, every)
        nc.sync.dma_start(out=x_raw[:], in_=x.rearrange("(p j) t -> p j t", j=PACK))
        nc.sync.dma_start(out=w0_raw[:].bitcast(I32), in_=w0_words[0].bitcast(I32))
        load_w2(w2_first, 0, 2)
        load_scale_rows(1, w1_scales, W1_ROW, [0])
        deal_scales(0, 0, 3)
        cast_x(on_vector, 0, D)
        cast_x(on_scalar, D, T)
        load_scale_rows(1, w1_scales, W1_ROW, [1, 2, 3])
        nc.sync.dma_start(out=w1_raw[:], in_=w1_words[0].rearrange("p n i -> p (n i)").bitcast(I32))
        load_g(0)
        load_g(1)
        load_w2(w2_last, 2, 3)
        load_g(2)

        cast_x(on_scalar, T, XW)
        deal_w0(0, 3)
        quantize_x(0)
        open_with_w0(0, every)
        open_with_w0(1, every)
        quantize_x(1)
        cast_w2(on_vector, 0, 0, 84)
        cast_w2(on_scalar, 0, 84, P)
        deal_scales(1, 0, 1)
        quantize_w2(0)
        cast_w2(on_vector, 1, 0, 84)
        cast_w2(on_scalar, 1, 84, P)
        deal_scales(1, 1, 2)
        quantize_w2(1)
        deal_scales(1, 2, 3)
        for a in range(NCH):
            deal_w1(on_scalar, a, a + 1)
        w2_pass(0, every, False)
        w1_pass(0, every, True)
        for r in every:
            w2_pass(1, [r], False)
            w1_pass(1, [r], True)
        park(0, 0)
        for t0 in (0, HALF):
            gate_parked(0, 0, t0, t0 + HALF)
        park(1, 0)
        gate(0, range(1, 3))
        for t0 in (0, HALF):
            gate(0, [3], t0, t0 + HALF)
            cast_y(on_scalar, 0, t0, t0 + HALF)
        store_y(nc.sync, 0, 1)
        gate_parked(1, 0)
        gate(1, range(1, 4))
        store_y(nc.sync, 1, 2)
        for r in every:
            open_with_w0(2, [r])
            w1_pass(2, [r], False)
        quantize_y(0, 0, HALF)
        cast_w2(on_scalar, 2, 84, P)
        cast_w2(on_vector, 2, 0, 84)
        quantize_w2(2, 0, CH // 2)
        quantize_w2(2, CH // 2, CH)
        w2_pass(2, every, True)
        quantize_y(0, HALF, T)
        cast_y(on_scalar, 1, 0, P)
        park(2, 0, 0, 416)
        gate_parked(2, 0, 0, 416)
        cast_y(on_scalar, 1, P, T)
        gate(2, range(1, 4))
        gate(2, [0], 416, T)
        store_y(nc.sync, 2, 3)
        cast_y(on_scalar, 2, 320, T)
        cast_y(on_vector, 2, 0, 320)
        quantize_y(1)
        quantize_y(2)
        store_codes(nc.sync, 0, 3)
        for r in range(4):
            nc.sync.dma_start(
                out=out_2[:, r:16:4, :].rearrange("a q t -> q a t").bitcast(I32),
                in_=o_scales[OUT_ROW + r : P : 32, :, :].bitcast(I32),
            )
